import numpy as np
import ml_dtypes


def mxq(x, axis, fmt="e4m3"):
    dtype, down = {"e4m3": (ml_dtypes.float8_e4m3fn, 7), "e5m2": (ml_dtypes.float8_e5m2, 14)}[fmt]
    v = np.moveaxis(np.asarray(x, np.float32).astype(ml_dtypes.bfloat16).astype(np.float64), axis, -1)
    blocks = v.reshape(v.shape[:-1] + (-1, 32))
    amax = np.abs(blocks).max(-1, keepdims=True)
    byte = np.maximum(np.where(amax > 0, np.frexp(amax)[1] - 1 + 127, 0) - down, 1)
    scale = np.exp2(byte - 127.0)
    codes = (blocks / scale).astype(np.float32).astype(dtype).astype(np.float64)
    return np.moveaxis((codes * scale).reshape(v.shape), -1, axis)


WIDE = False


def mx_kscale(k):
    if not WIDE:
        return np.ones(k)
    levels = np.array([10, -10, 5, -5, 0])
    if k % 512:
        return np.exp2(np.random.permutation(np.resize(levels, k // 32))).repeat(32)
    a = np.empty((k // 512, 16))
    for p in range(k // 512):
        a[p, :8] = np.random.permutation(np.resize(levels, 8))
        for g in range(8):
            far = levels[np.abs(levels - a[p, g]) >= 10]
            a[p, g + 8] = far[np.random.randint(len(far))]
    return np.exp2(a.ravel()).repeat(32)


BF16 = ml_dtypes.bfloat16


def bf(x):
    return np.asarray(x, np.float32).astype(BF16)


def f64(x):
    return np.asarray(x).astype(np.float64)


P, K, T, C = 1024, 1024, 2048, 512

PHASE_STD = 0.45
ONSET_STD = 0.2
AMP_SPREAD = 0.3


def draw0():
    s = mx_kscale(K)
    t = mx_kscale(P)
    freq = np.random.standard_normal((P, K)) * PHASE_STD * s
    basis = np.random.standard_normal((K, T)) / np.sqrt(K) / s[:, None]
    onset = np.random.standard_normal(P) * ONSET_STD
    amp = (1 + AMP_SPREAD * np.random.standard_normal(P)) * t
    mix = 2 * np.random.standard_normal((C, P)) / np.sqrt(P) / t
    return {"freq": bf(freq), "basis": bf(basis), "onset": bf(onset),
            "amp": bf(amp), "mix": bf(mix)}


def core(freq, basis, onset, amp, mix):
    phase = mxq(f64(freq), 1, "e4m3") @ mxq(f64(basis), 0, "e4m3")
    wave = np.sin(phase + f64(onset)[:, None]) * f64(amp)[:, None]
    y = mxq(f64(mix), 1, "e4m3") @ mxq(wave, 0, "e4m3")
    return y


def e4m3fn_bytes(y):
    return np.clip(np.asarray(y, np.float64), -448.0, 448.0).astype(np.float32).astype(ml_dtypes.float8_e4m3fn).view(np.uint8)


def e4m3fn_values(b):
    return np.asarray(b, np.uint8).view(ml_dtypes.float8_e4m3fn).astype(np.float64)


def setup_inputs():
    d = draw0()
    x0 = np.asarray(d['basis']).astype(np.float64)
    s = (np.max(np.abs(x0), axis=(1,), keepdims=True) / 448.0).astype(np.float32)
    out = {}
    for k, v in d.items():
        if k == 'basis':
            out['basis_bytes'] = e4m3fn_bytes(x0 / s.astype(np.float64))
            out['basis_scale'] = s
        else:
            out[k] = v
    return out


def reference(freq, basis_bytes, basis_scale, onset, amp, mix):
    return core(freq, e4m3fn_values(basis_bytes) * basis_scale.astype(np.float64), onset, amp, mix)

@@ -1,0 +1,357 @@
+from contextlib import ExitStack
+
+import concourse.mybir as mybir
+from concourse.masks import make_identity
+
+P, K, T, C = 1024, 1024, 2048, 512
+FLOPS = 2 * P * K * T + 2 * C * P * T
+
+F32 = mybir.dt.float32
+BF16 = mybir.dt.bfloat16
+U32 = mybir.dt.uint32
+U8 = mybir.dt.uint8
+FP8 = mybir.dt.float8_e4m3fn
+FP8X4 = mybir.dt.float8_e4m3fn_x4
+MULT = mybir.AluOpType.mult
+ADD = mybir.AluOpType.add
+ACTF = mybir.ActivationFunctionType
+
+PART = 128
+CH = 512
+NCH = T // CH
+NSTEP = 2 * NCH
+PH = 3
+ND = [3,2,2,2,2,2,2,1]
+XG = [0,0,0,320,320,320,320,320]
+
+
+def tile_additive_sine_synthesis_s7_kernel(
+    tc, freq, basis_bytes, basis_scale, onset, amp, mix, out
+):
+    nc = tc.nc
+    with ExitStack() as ctx:
+        keep = ctx.enter_context(tc.tile_pool(name="keep", bufs=1))
+        work = ctx.enter_context(tc.tile_pool(name="work", bufs=3))
+        psum = ctx.enter_context(tc.psum_pool(name="psum", bufs=4))
+        ctx.enter_context(tc.manual_schedule())
+
+        ident = keep.tile([PART, PART], F32, name="ident")
+        ident_bf = keep.tile([PART, PART], BF16, name="ident_bf")
+        dummy = keep.tile([PART, 1], F32, name="dummy")
+        sc = keep.tile([PART, 2, 4], F32, name="sc")
+        on_bf = keep.tile([PART, 2, 4], BF16, name="on_bf")
+        am_bf = keep.tile([PART, 2, 4], BF16, name="am_bf")
+        on = keep.tile([PART, 2, 4], F32, name="on")
+        am = psum.tile([PART, 2, 4], F32, name="am", tag="am", bufs=1)
+        raw = [keep.tile([PART, 2, 4, CH], U8, name="raw%d" % c) for c in range(NCH)]
+        fx = keep.tile([PART, 8, K], BF16, name="fx", align_bytes=64)
+        mx = keep.tile([PART, 4, P], BF16, name="mx", align_bytes=64)
+        fc = keep.tile([PART, 8, 2 * PART], U32, name="fc", align_bytes=64)
+        fs = keep.tile([PART, 8, 2 * PART], U8, name="fs", align_bytes=64)
+        mc = keep.tile([PART, 4, 2 * PART], U32, name="mc", align_bytes=64)
+        ms = keep.tile([PART, 4, 2 * PART], U8, name="ms", align_bytes=64)
+        bc = keep.tile([PART, NSTEP, CH], U32, name="bc", align_bytes=64)
+        bs = keep.tile([PART, NSTEP, CH], U8, name="bs", align_bytes=64)
+
+        basis_v = basis_bytes.rearrange("(g p t) n -> g p t n", p=PART, t=4)
+        freq_v = freq.rearrange("(h m t) k -> h t m k", m=PART, t=4)
+        mix_v = mix.rearrange("(c m) k -> c m k", m=PART)
+
+        def load_basis(c):
+            for g in range(2):
+                nc.sync.dma_start(out=raw[c][:, g, :, :], in_=basis_v[g, :, :, c * CH : (c + 1) * CH])
+
+        def load_freq(i):
+            nc.sync.dma_start(out=fx[:, i, :], in_=freq_v[i // 4, i % 4])
+
+        nc.scalar.dma_start(out=sc[:], in_=basis_scale.rearrange("(g p t) o -> p g (t o)", p=PART, t=4))
+        nc.scalar.dma_start(out=on_bf[:], in_=onset.rearrange("(g p t) -> p g t", p=PART, t=4))
+        nc.scalar.dma_start(out=am_bf[:], in_=amp.rearrange("(g p t) -> p g t", p=PART, t=4))
+        load_basis(0)
+        for i in range(4):
+            load_freq(i)
+        load_basis(1)
+        for i in range(4, 8):
+            load_freq(i)
+        for c in range(4):
+            nc.sync.dma_start(out=mx[:, c, :], in_=mix_v[c])
+        load_basis(2)
+        load_basis(3)
+
+        nc.gpsimd.memset(dummy[:], 0.0)
+        make_identity(nc, ident[:])
+        make_identity(nc, ident_bf[:])
+        nc.scalar.activation(out=dummy[:], in_=dummy[:], func=ACTF.Sin)
+
+        wid = {}
+        inter = {}
+        tr = {}
+        grouped = {}
+        ph = {}
+        sn = {}
+        wb = {}
+        wc = {}
+        ws = {}
+        yo = {}
+
+        def widen(b, planes, engine):
+            if b >= NSTEP:
+                return
+            if b not in wid:
+                wid[b] = work.tile([PART, 4, CH], BF16, name="wid", tag="wid", align_bytes=64)
+            c, g = b // 2, b % 2
+            for t in planes:
+                src = raw[c][:, g, t, :].bitcast(FP8)
+                if engine == "v":
+                    nc.vector.tensor_scalar(
+                        out=wid[b][:, t, :], in0=src, scalar1=sc[:, g, t : t + 1], scalar2=None, op0=MULT
+                    )
+                else:
+                    nc.scalar.activation(out=wid[b][:, t, :], in_=src, func=ACTF.Copy, scale=sc[:, g, t : t + 1])
+
+        def interleave(b, n0, n1):
+            if b >= NSTEP:
+                return
+            if b not in inter:
+                inter[b] = work.tile([PART, CH, 4], BF16, name="inter", tag="inter", align_bytes=64)
+            nc.vector.tensor_copy(
+                out=inter[b][:, n0:n1, :].rearrange("p (c i) t -> p c t i", i=4),
+                in_=wid[b][:, :, n0:n1].rearrange("p t (c i) -> p c t i", i=4),
+            )
+
+        def interleave_gp(b, n0, n1):
+            if b >= NSTEP or n1 == n0:
+                return
+            if b not in inter:
+                inter[b] = work.tile([PART, CH, 4], BF16, name="inter", tag="inter", align_bytes=64)
+            nc.gpsimd.tensor_scalar(
+                out=inter[b][:, n0:n1, :],
+                in0=wid[b][:, :, n0:n1].rearrange("p t n -> p n t"),
+                scalar1=1.0,
+                scalar2=0.0,
+                op0=MULT,
+                op1=ADD,
+            )
+
+        def quant_basis(b):
+            if b >= NSTEP:
+                return
+            nc.vector.quantize_mx(
+                out=bc[:, b, :].bitcast(FP8X4), scales=bs[:, b, :], in_=inter[b][:].rearrange("p n t -> p (n t)")
+            )
+
+        def turn(key, rows):
+            words = rows.bitcast(F32)
+            tr[key] = psum.tile([PART, 2, 2, PART], F32, name="mo", tag="mo")
+            for g in range(2):
+                for u in range(2):
+                    nc.tensor.transpose(
+                        tr[key][:, g, u, :], words[:, 256 * g + u : 256 * (g + 1) : 2], ident[:]
+                    )
+
+        def turn_out(key):
+            grouped[key] = work.tile([PART, 2, PART, 4], BF16, name="grouped", tag="grouped", align_bytes=64, bufs=4)
+            nc.scalar.copy(
+                out=grouped[key][:].rearrange("p g r t -> p (g r t)").bitcast(F32).rearrange(
+                    "p (g r u) -> p g r u", g=2, u=2
+                ),
+                in_=tr[key][:].rearrange("p g u r -> p g r u"),
+            )
+
+        def turn_quant(key, codes, scales):
+            nc.vector.quantize_mx(
+                out=codes.bitcast(FP8X4), scales=scales, in_=grouped[key][:].rearrange("p g r t -> p (g r t)")
+            )
+
+        def phase_mm(h):
+            if h >= NSTEP:
+                return
+            c, half = h // 2, h % 2
+            for t in range(4):
+                ph[h, t] = psum.tile([PART, CH], F32, name="ph", tag="ph", bufs=PH)
+                i = 4 * half + t
+                for g in range(2):
+                    nc.tensor.matmul_mx(
+                        out=ph[h, t][:],
+                        lhsT=fc[:, i, PART * g : PART * (g + 1)].bitcast(FP8X4),
+                        lhsT_scale=fs[:, i, PART * g : PART * (g + 1)],
+                        rhs=bc[:, 2 * c + g, :].bitcast(FP8X4),
+                        rhs_scale=bs[:, 2 * c + g, :],
+                        start=(g == 0),
+                        stop=(g == 1),
+                    )
+
+        def sines(h):
+            if h >= NSTEP:
+                return
+            sn[h] = work.tile([PART, 4, CH], F32, name="sn", tag="sn")
+            for t in range(4):
+                nc.scalar.activation(
+                    out=sn[h][:, t, :], in_=ph[h, t][:], func=ACTF.Sin, bias=on[:, h % 2, t : t + 1]
+                )
+
+        def amplify(h, n0=0, n1=CH):
+            if h not in wb:
+                wb[h] = work.tile([PART, CH, 4], BF16, name="wb", tag="wb", align_bytes=64)
+            nc.vector.tensor_tensor(
+                out=wb[h][:, n0:n1, :].rearrange("p (c i) t -> p c t i", i=4),
+                in0=sn[h][:, :, n0:n1].rearrange("p t (c i) -> p c t i", i=4),
+                in1=am[:, h % 2, :]
+                .rearrange("p (c t i) -> p c t i", c=1, i=1)
+                .to_broadcast([PART, (n1 - n0) // 4, 4, 4]),
+                op=MULT,
+            )
+
+        def quant_wave(h, n0=0, n1=CH):
+            if h not in wc:
+                wc[h] = work.tile([PART, CH], U32, name="wc", tag="wc", align_bytes=64, bufs=4)
+                ws[h] = work.tile([PART, CH], U8, name="ws", tag="ws", align_bytes=64, bufs=4)
+            nc.vector.quantize_mx(
+                out=wc[h][:, n0:n1].bitcast(FP8X4),
+                scales=ws[h][:, n0:n1],
+                in_=wb[h][:, n0:n1, :].rearrange("p n t -> p (n t)"),
+            )
+
+        def mix_pass(key, m, h, n0, n1, start, stop, tag="mo"):
+            if start:
+                if tag == "mo":
+                    yo[key, m] = psum.tile([PART, CH], F32, name="mo", tag="mo")
+                else:
+                    yo[key, m] = psum.tile([PART, CH], F32, name="ph", tag="ph", bufs=PH)
+            half = h % 2
+            nc.tensor.matmul_mx(
+                out=yo[key, m][:, 0 : n1 - n0],
+                lhsT=mc[:, m, PART * half : PART * (half + 1)].bitcast(FP8X4),
+                lhsT_scale=ms[:, m, PART * half : PART * (half + 1)],
+                rhs=wc[h][:, n0:n1].bitcast(FP8X4),
+                rhs_scale=ws[h][:, n0:n1],
+                start=start,
+                stop=stop,
+            )
+
+        def mix_chunk(c):
+            for m in range(4):
+                mix_pass(c, m, 2 * c, 0, CH, True, False)
+                mix_pass(c, m, 2 * c + 1, 0, CH, False, True)
+
+        def emit(key, m, col, width, engine):
+            res = work.tile([PART, CH], F32, name="res", tag="res", bufs=8)
+            if engine == "v":
+                nc.vector.tensor_copy(out=res[:, 0:width], in_=yo[key, m][:, 0:width])
+            else:
+                nc.scalar.copy(out=res[:, 0:width], in_=yo[key, m][:, 0:width])
+            nc.sync.dma_start(out=out[PART * m : PART * (m + 1), col : col + width], in_=res[:, 0:width])
+
+        def wv(b):
+            if b < NSTEP:
+                widen(b, range(0, ND[b]), "v")
+
+        def wa(b):
+            if b < NSTEP:
+                widen(b, range(ND[b], 4), "s")
+
+        def iv(b):
+            if b < NSTEP:
+                interleave(b, 0, CH - XG[b])
+
+        def ig(b):
+            if b < NSTEP:
+                interleave_gp(b, CH - XG[b], CH)
+
+        def fq(i):
+            turn_quant(("f", i), fc[:, i, :], fs[:, i, :])
+
+        def mq(c):
+            turn_quant(("m", c), mc[:, c, :], ms[:, c, :])
+
+        wv(0)
+        wa(0)
+        wv(1)
+        wa(1)
+        nc.vector.tensor_copy(out=on[:], in_=on_bf[:])
+        nc.tensor.matmul(
+            am[:].rearrange("p g t -> p (g t)"),
+            lhsT=ident_bf[:],
+            rhs=am_bf[:].rearrange("p g t -> p (g t)"),
+            start=True,
+            stop=True,
+        )
+        for i in range(4):
+            turn(("f", i), fx[:, i, :])
+            turn_out(("f", i))
+        iv(0)
+        iv(1)
+        quant_basis(0)
+        fq(0)
+        fq(1)
+        quant_basis(1)
+        wv(2)
+        wa(2)
+        fq(2)
+        fq(3)
+        wa(3)
+        for i in range(4, 8):
+            turn(("f", i), fx[:, i, :])
+            turn_out(("f", i))
+        phase_mm(0)
+        iv(2)
+        sines(0)
+        for i in range(8, 8):
+            turn(("f", i), fx[:, i, :])
+            turn_out(("f", i))
+        fq(4)
+        fq(5)
+        quant_basis(2)
+        fq(6)
+        fq(7)
+
+        for h in range(NSTEP - 1):
+            wv(h + 3)
+            ig(h + 3)
+            amplify(h)
+            phase_mm(h + 1)
+            if h >= 2 and h % 2 == 0:
+                mix_chunk(h // 2 - 1)
+            if h > 0:
+                wa(h + 4)
+            sines(h + 1)
+            if h == 0:
+                wa(h + 4)
+            if h < 2:
+                for c in (2 * h, 2 * h + 1):
+                    turn(("m", c), mx[:, c, :])
+                    turn_out(("m", c))
+            iv(h + 3)
+            if h == 1:
+                mq(0)
+                mq(1)
+            if h >= 2:
+                c = h // 2 - 1
+                for m in (2 * (h % 2), 2 * (h % 2) + 1):
+                    emit(c, m, c * CH, CH, "s"[m % 1])
+            quant_wave(h)
+            quant_basis(h + 3)
+            if h == 1:
+                mq(2)
+                mq(3)
+
+        h = NSTEP - 1
+        last = NCH - 1
+        halves = ((0, CH // 2), (CH // 2, CH))
+        for j, (n0, n1) in enumerate(halves):
+            for m in range(4):
+                if j == 0 or m < PH:
+                    mix_pass((last, j), m, h - 1, n0, n1, True, False, "mo" if j == 0 else "ph")
+        for n0, n1 in halves:
+            amplify(h, n0, n1)
+        emit(last - 1, 2, (last - 1) * CH, CH, "s")
+        emit(last - 1, 3, (last - 1) * CH, CH, "s")
+        for n0, n1 in halves:
+            quant_wave(h, n0, n1)
+        for j, (n0, n1) in enumerate(halves):
+            for m in range(4):
+                if j == 1 and m >= PH:
+                    mix_pass((last, j), m, h - 1, n0, n1, True, False)
+                mix_pass((last, j), m, h, n0, n1, False, True)
+            for m in range(4):
+                emit((last, j), m, last * CH + n0, n1 - n0, "vs"[m % 2])

@@ -19,10 +19,12 @@ ACTF = mybir.ActivationFunctionType
 PART = 128
 CH = 512
 NCH = T // CH
-NSTEP = 2 * NCH
+NB = 2 * NCH
 PH = 3
-ND = [3,2,2,2,2,2,2,1]
-XG = [0,0,0,320,320,320,320,320]
+SN = 4
+LEAD = 4
+XG = 288
+VA = 384
 
 
 def tile_additive_sine_synthesis_s7_kernel(
@@ -39,49 +41,34 @@ def tile_additive_sine_synthesis_s7_kernel(
         ident_bf = keep.tile([PART, PART], BF16, name="ident_bf")
         dummy = keep.tile([PART, 1], F32, name="dummy")
         sc = keep.tile([PART, 2, 4], F32, name="sc")
-        on_bf = keep.tile([PART, 2, 4], BF16, name="on_bf")
+        on = keep.tile([PART, 2, 4], BF16, name="on")
         am_bf = keep.tile([PART, 2, 4], BF16, name="am_bf")
-        on = keep.tile([PART, 2, 4], F32, name="on")
         am = psum.tile([PART, 2, 4], F32, name="am", tag="am", bufs=1)
-        raw = [keep.tile([PART, 2, 4, CH], U8, name="raw%d" % c) for c in range(NCH)]
-        fx = keep.tile([PART, 8, K], BF16, name="fx", align_bytes=64)
-        mx = keep.tile([PART, 4, P], BF16, name="mx", align_bytes=64)
+        raw = [[keep.tile([PART, 2, CH], U8, name="raw%d_%d" % (b, u)) for u in range(2)] for b in range(NB)]
+        fx = [keep.tile([PART, K], BF16, name="fx%d" % i, align_bytes=64) for i in range(8)]
+        mx = [keep.tile([PART, P], BF16, name="mx%d" % c, align_bytes=64) for c in range(4)]
         fc = keep.tile([PART, 8, 2 * PART], U32, name="fc", align_bytes=64)
         fs = keep.tile([PART, 8, 2 * PART], U8, name="fs", align_bytes=64)
         mc = keep.tile([PART, 4, 2 * PART], U32, name="mc", align_bytes=64)
         ms = keep.tile([PART, 4, 2 * PART], U8, name="ms", align_bytes=64)
-        bc = keep.tile([PART, NSTEP, CH], U32, name="bc", align_bytes=64)
-        bs = keep.tile([PART, NSTEP, CH], U8, name="bs", align_bytes=64)
+        bc = keep.tile([PART, NB, CH], U32, name="bc", align_bytes=64)
+        bs = keep.tile([PART, NB, CH], U8, name="bs", align_bytes=64)
 
         basis_v = basis_bytes.rearrange("(g p t) n -> g p t n", p=PART, t=4)
         freq_v = freq.rearrange("(h m t) k -> h t m k", m=PART, t=4)
         mix_v = mix.rearrange("(c m) k -> c m k", m=PART)
+        out_v = out.rearrange("(m p) n -> p m n", p=PART)
 
-        def load_basis(c):
-            for g in range(2):
-                nc.sync.dma_start(out=raw[c][:, g, :, :], in_=basis_v[g, :, :, c * CH : (c + 1) * CH])
+        def load_basis(b):
+            c, g = b // 2, b % 2
+            for u in range(2):
+                nc.sync.dma_start(out=raw[b][u][:], in_=basis_v[g, :, 2 * u : 2 * u + 2, c * CH : (c + 1) * CH])
 
         def load_freq(i):
-            nc.sync.dma_start(out=fx[:, i, :], in_=freq_v[i // 4, i % 4])
+            nc.sync.dma_start(out=fx[i][:], in_=freq_v[i // 4, i % 4])
 
-        nc.scalar.dma_start(out=sc[:], in_=basis_scale.rearrange("(g p t) o -> p g (t o)", p=PART, t=4))
-        nc.scalar.dma_start(out=on_bf[:], in_=onset.rearrange("(g p t) -> p g t", p=PART, t=4))
-        nc.scalar.dma_start(out=am_bf[:], in_=amp.rearrange("(g p t) -> p g t", p=PART, t=4))
-        load_basis(0)
-        for i in range(4):
-            load_freq(i)
-        load_basis(1)
-        for i in range(4, 8):
-            load_freq(i)
-        for c in range(4):
-            nc.sync.dma_start(out=mx[:, c, :], in_=mix_v[c])
-        load_basis(2)
-        load_basis(3)
-
-        nc.gpsimd.memset(dummy[:], 0.0)
-        make_identity(nc, ident[:])
-        make_identity(nc, ident_bf[:])
-        nc.scalar.activation(out=dummy[:], in_=dummy[:], func=ACTF.Sin)
+        def load_mix(c):
+            nc.sync.dma_start(out=mx[c][:], in_=mix_v[c])
 
         wid = {}
         inter = {}
@@ -95,13 +82,11 @@ def tile_additive_sine_synthesis_s7_kernel(
         yo = {}
 
         def widen(b, planes, engine):
-            if b >= NSTEP:
-                return
             if b not in wid:
                 wid[b] = work.tile([PART, 4, CH], BF16, name="wid", tag="wid", align_bytes=64)
-            c, g = b // 2, b % 2
+            g = b % 2
             for t in planes:
-                src = raw[c][:, g, t, :].bitcast(FP8)
+                src = raw[b][t // 2][:, t % 2, :].bitcast(FP8)
                 if engine == "v":
                     nc.vector.tensor_scalar(
                         out=wid[b][:, t, :], in0=src, scalar1=sc[:, g, t : t + 1], scalar2=None, op0=MULT
@@ -109,21 +94,22 @@ def tile_additive_sine_synthesis_s7_kernel(
                 else:
                     nc.scalar.activation(out=wid[b][:, t, :], in_=src, func=ACTF.Copy, scale=sc[:, g, t : t + 1])
 
+        def new_inter(b):
+            if b < LEAD:
+                return work.tile([PART, CH, 4], BF16, name="inter", tag="inter", align_bytes=64, bufs=2)
+            return work.tile([PART, CH, 4], BF16, name="shared", tag="shared", align_bytes=64, bufs=1)
+
         def interleave(b, n0, n1):
-            if b >= NSTEP:
-                return
             if b not in inter:
-                inter[b] = work.tile([PART, CH, 4], BF16, name="inter", tag="inter", align_bytes=64)
+                inter[b] = new_inter(b)
             nc.vector.tensor_copy(
                 out=inter[b][:, n0:n1, :].rearrange("p (c i) t -> p c t i", i=4),
                 in_=wid[b][:, :, n0:n1].rearrange("p t (c i) -> p c t i", i=4),
             )
 
         def interleave_gp(b, n0, n1):
-            if b >= NSTEP or n1 == n0:
-                return
             if b not in inter:
-                inter[b] = work.tile([PART, CH, 4], BF16, name="inter", tag="inter", align_bytes=64)
+                inter[b] = new_inter(b)
             nc.gpsimd.tensor_scalar(
                 out=inter[b][:, n0:n1, :],
                 in0=wid[b][:, :, n0:n1].rearrange("p t n -> p n t"),
@@ -133,11 +119,11 @@ def tile_additive_sine_synthesis_s7_kernel(
                 op1=ADD,
             )
 
-        def quant_basis(b):
-            if b >= NSTEP:
-                return
+        def quant_basis(b, n0=0, n1=CH):
             nc.vector.quantize_mx(
-                out=bc[:, b, :].bitcast(FP8X4), scales=bs[:, b, :], in_=inter[b][:].rearrange("p n t -> p (n t)")
+                out=bc[:, b, n0:n1].bitcast(FP8X4),
+                scales=bs[:, b, n0:n1],
+                in_=inter[b][:, n0:n1, :].rearrange("p n t -> p (n t)"),
             )
 
         def turn(key, rows):
@@ -149,25 +135,41 @@ def tile_additive_sine_synthesis_s7_kernel(
                         tr[key][:, g, u, :], words[:, 256 * g + u : 256 * (g + 1) : 2], ident[:]
                     )
 
-        def turn_out(key):
+        def turn_out(key, engine="s"):
             grouped[key] = work.tile([PART, 2, PART, 4], BF16, name="grouped", tag="grouped", align_bytes=64, bufs=4)
-            nc.scalar.copy(
-                out=grouped[key][:].rearrange("p g r t -> p (g r t)").bitcast(F32).rearrange(
-                    "p (g r u) -> p g r u", g=2, u=2
-                ),
-                in_=tr[key][:].rearrange("p g u r -> p g r u"),
+            dst = grouped[key][:].rearrange("p g r t -> p (g r t)").bitcast(F32).rearrange(
+                "p (g r u) -> p g r u", g=2, u=2
             )
+            src = tr[key][:].rearrange("p g u r -> p g r u")
+            if engine == "s":
+                nc.scalar.copy(out=dst, in_=src)
+            else:
+                nc.vector.tensor_copy(out=dst, in_=src)
 
         def turn_quant(key, codes, scales):
             nc.vector.quantize_mx(
                 out=codes.bitcast(FP8X4), scales=scales, in_=grouped[key][:].rearrange("p g r t -> p (g r t)")
             )
 
-        def phase_mm(h):
-            if h >= NSTEP:
-                return
+        def tf(i, engine="s"):
+            turn(("f", i), fx[i][:])
+            turn_out(("f", i), engine)
+
+        def tm(c, engine="s"):
+            turn(("m", c), mx[c][:])
+            turn_out(("m", c), engine)
+
+        def fq(i):
+            turn_quant(("f", i), fc[:, i, :], fs[:, i, :])
+
+        def mq(c):
+            turn_quant(("m", c), mc[:, c, :], ms[:, c, :])
+
+        def sines(h, planes=range(4)):
             c, half = h // 2, h % 2
-            for t in range(4):
+            if h not in sn:
+                sn[h] = work.tile([PART, 4, CH], F32, name="sn", tag="sn", bufs=SN)
+            for t in planes:
                 ph[h, t] = psum.tile([PART, CH], F32, name="ph", tag="ph", bufs=PH)
                 i = 4 * half + t
                 for g in range(2):
@@ -180,25 +182,27 @@ def tile_additive_sine_synthesis_s7_kernel(
                         start=(g == 0),
                         stop=(g == 1),
                     )
-
-        def sines(h):
-            if h >= NSTEP:
-                return
-            sn[h] = work.tile([PART, 4, CH], F32, name="sn", tag="sn")
-            for t in range(4):
                 nc.scalar.activation(
-                    out=sn[h][:, t, :], in_=ph[h, t][:], func=ACTF.Sin, bias=on[:, h % 2, t : t + 1]
+                    out=sn[h][:, t, :], in_=ph[h, t][:], func=ACTF.Sin, bias=on[:, half, t : t + 1]
                 )
 
         def amplify(h, n0=0, n1=CH):
-            if h not in wb:
-                wb[h] = work.tile([PART, CH, 4], BF16, name="wb", tag="wb", align_bytes=64)
+            w = n1 - n0
+            wb[h, n0] = work.tile([PART, w, 4], BF16, name="wb", tag="wb", align_bytes=64, bufs=4)
             nc.vector.tensor_tensor(
-                out=wb[h][:, n0:n1, :].rearrange("p (c i) t -> p c t i", i=4),
+                out=wb[h, n0][:].rearrange("p (c i) t -> p c t i", i=4),
                 in0=sn[h][:, :, n0:n1].rearrange("p t (c i) -> p c t i", i=4),
-                in1=am[:, h % 2, :]
-                .rearrange("p (c t i) -> p c t i", c=1, i=1)
-                .to_broadcast([PART, (n1 - n0) // 4, 4, 4]),
+                in1=am[:, h % 2, :].rearrange("p (c t i) -> p c t i", c=1, i=1).to_broadcast([PART, w // 4, 4, 4]),
+                op=MULT,
+            )
+
+        def amplify_gp(h, n0, n1):
+            w = n1 - n0
+            wb[h, n0] = work.tile([PART, w, 4], BF16, name="shared", tag="shared", align_bytes=64, bufs=1)
+            nc.gpsimd.tensor_tensor(
+                out=wb[h, n0][:],
+                in0=sn[h][:, :, n0:n1].rearrange("p t n -> p n t"),
+                in1=am_bf[:, h % 2, :].rearrange("p (n t) -> p n t", n=1).to_broadcast([PART, w, 4]),
                 op=MULT,
             )
 
@@ -209,18 +213,13 @@ def tile_additive_sine_synthesis_s7_kernel(
             nc.vector.quantize_mx(
                 out=wc[h][:, n0:n1].bitcast(FP8X4),
                 scales=ws[h][:, n0:n1],
-                in_=wb[h][:, n0:n1, :].rearrange("p n t -> p (n t)"),
+                in_=wb[h, n0][:].rearrange("p n t -> p (n t)"),
             )
 
-        def mix_pass(key, m, h, n0, n1, start, stop, tag="mo"):
-            if start:
-                if tag == "mo":
-                    yo[key, m] = psum.tile([PART, CH], F32, name="mo", tag="mo")
-                else:
-                    yo[key, m] = psum.tile([PART, CH], F32, name="ph", tag="ph", bufs=PH)
+        def mix_pass(dst, m, h, n0, n1, start, stop):
             half = h % 2
             nc.tensor.matmul_mx(
-                out=yo[key, m][:, 0 : n1 - n0],
+                out=dst,
                 lhsT=mc[:, m, PART * half : PART * (half + 1)].bitcast(FP8X4),
                 lhsT_scale=ms[:, m, PART * half : PART * (half + 1)],
                 rhs=wc[h][:, n0:n1].bitcast(FP8X4),
@@ -229,129 +228,165 @@ def tile_additive_sine_synthesis_s7_kernel(
                 stop=stop,
             )
 
-        def mix_chunk(c):
-            for m in range(4):
-                mix_pass(c, m, 2 * c, 0, CH, True, False)
-                mix_pass(c, m, 2 * c + 1, 0, CH, False, True)
-
-        def emit(key, m, col, width, engine):
-            res = work.tile([PART, CH], F32, name="res", tag="res", bufs=8)
-            if engine == "v":
-                nc.vector.tensor_copy(out=res[:, 0:width], in_=yo[key, m][:, 0:width])
+        def mix_bank(c, rows, n0=0, n1=CH, tag="mo"):
+            key = (c, rows, n0)
+            if tag == "mo":
+                yo[key] = psum.tile([PART, len(rows), n1 - n0], F32, name="mo", tag="mo")
             else:
-                nc.scalar.copy(out=res[:, 0:width], in_=yo[key, m][:, 0:width])
-            nc.sync.dma_start(out=out[PART * m : PART * (m + 1), col : col + width], in_=res[:, 0:width])
+                yo[key] = psum.tile([PART, len(rows), n1 - n0], F32, name="ph", tag="ph", bufs=PH)
+            for j, m in enumerate(rows):
+                mix_pass(yo[key][:, j, :], m, 2 * c, n0, n1, True, False)
+                mix_pass(yo[key][:, j, :], m, 2 * c + 1, n0, n1, False, True)
 
-        def wv(b):
-            if b < NSTEP:
-                widen(b, range(0, ND[b]), "v")
+        def emit(c, rows, engine, n0=0, n1=CH):
+            res = work.tile([PART, len(rows), n1 - n0], F32, name="res", tag="res", bufs=8)
+            if engine == "v":
+                nc.vector.tensor_copy(out=res[:], in_=yo[c, rows, n0][:])
+            else:
+                nc.scalar.copy(out=res[:], in_=yo[c, rows, n0][:])
+            nc.sync.dma_start(out=out_v[:, rows[0] : rows[-1] + 1, c * CH + n0 : c * CH + n1], in_=res[:])
 
-        def wa(b):
-            if b < NSTEP:
-                widen(b, range(ND[b], 4), "s")
+        def out_rows(c, rows, engine, n0=0, n1=CH, tag="mo"):
+            mix_bank(c, rows, n0, n1, tag)
+            emit(c, rows, engine, n0, n1)
 
-        def iv(b):
-            if b < NSTEP:
-                interleave(b, 0, CH - XG[b])
+        nc.scalar.dma_start(out=sc[:], in_=basis_scale.rearrange("(g p t) o -> p g (t o)", p=PART, t=4))
+        nc.scalar.dma_start(out=on[:], in_=onset.rearrange("(g p t) -> p g t", p=PART, t=4))
+        nc.scalar.dma_start(out=am_bf[:], in_=amp.rearrange("(g p t) -> p g t", p=PART, t=4))
+        nc.gpsimd.memset(dummy[:], 0.0)
+        make_identity(nc, ident[:])
+        make_identity(nc, ident_bf[:])
+        nc.scalar.activation(out=dummy[:], in_=dummy[:], func=ACTF.Sin)
 
-        def ig(b):
-            if b < NSTEP:
-                interleave_gp(b, CH - XG[b], CH)
+        def amp_to_psum():
+            nc.tensor.matmul(
+                am[:].rearrange("p g t -> p (g t)"),
+                lhsT=ident_bf[:],
+                rhs=am_bf[:].rearrange("p g t -> p (g t)"),
+                start=True,
+                stop=True,
+            )
 
-        def fq(i):
-            turn_quant(("f", i), fc[:, i, :], fs[:, i, :])
-
-        def mq(c):
-            turn_quant(("m", c), mc[:, c, :], ms[:, c, :])
-
-        wv(0)
-        wa(0)
-        wv(1)
-        wa(1)
-        nc.vector.tensor_copy(out=on[:], in_=on_bf[:])
-        nc.tensor.matmul(
-            am[:].rearrange("p g t -> p (g t)"),
-            lhsT=ident_bf[:],
-            rhs=am_bf[:].rearrange("p g t -> p (g t)"),
-            start=True,
-            stop=True,
-        )
+        load_basis(0)
+        load_basis(1)
+        load_basis(2)
         for i in range(4):
-            turn(("f", i), fx[:, i, :])
-            turn_out(("f", i))
-        iv(0)
-        iv(1)
+            load_freq(i)
+        load_basis(3)
+        for i in range(4, 8):
+            load_freq(i)
+        load_basis(4)
+        load_basis(5)
+        for c in range(4):
+            load_mix(c)
+        load_basis(6)
+        load_basis(7)
+
+        widen(0, (0, 1), "v")
+        widen(0, (2, 3), "s")
+        widen(1, (0, 1, 2), "v")
+        widen(1, (3,), "s")
+        widen(2, (0, 1, 2), "s")
+        tf(0)
+        widen(2, (3,), "s")
+        tf(1)
+        tf(2)
+        tf(3)
+        amp_to_psum()
+        interleave(0, 0, CH)
+        interleave(1, 0, CH)
         quant_basis(0)
         fq(0)
-        fq(1)
         quant_basis(1)
-        wv(2)
-        wa(2)
+        fq(1)
+        widen(3, (0, 1), "v")
         fq(2)
+        interleave(2, 0, CH)
         fq(3)
-        wa(3)
-        for i in range(4, 8):
-            turn(("f", i), fx[:, i, :])
-            turn_out(("f", i))
-        phase_mm(0)
-        iv(2)
-        sines(0)
-        for i in range(8, 8):
-            turn(("f", i), fx[:, i, :])
-            turn_out(("f", i))
-        fq(4)
-        fq(5)
         quant_basis(2)
-        fq(6)
-        fq(7)
+        widen(3, (2,), "s")
+        sines(0, (0,))
+        widen(3, (3,), "s")
+        sines(0, (1, 2))
+        for i in range(4, 8):
+            tf(i)
+        sines(0, (3,))
+        interleave(3, 0, CH)
+        widen(4, (0, 1), "v")
+        quant_basis(3)
+        for i in range(4, 8):
+            fq(i)
+        widen(4, (2, 3), "v")
 
-        for h in range(NSTEP - 1):
-            wv(h + 3)
-            ig(h + 3)
+        def step(h, planes):
+            b = h + LEAD
+            interleave_gp(b, CH - XG, CH)
             amplify(h)
-            phase_mm(h + 1)
-            if h >= 2 and h % 2 == 0:
-                mix_chunk(h // 2 - 1)
-            if h > 0:
-                wa(h + 4)
-            sines(h + 1)
-            if h == 0:
-                wa(h + 4)
-            if h < 2:
-                for c in (2 * h, 2 * h + 1):
-                    turn(("m", c), mx[:, c, :])
-                    turn_out(("m", c))
-            iv(h + 3)
-            if h == 1:
-                mq(0)
-                mq(1)
-            if h >= 2:
-                c = h // 2 - 1
-                for m in (2 * (h % 2), 2 * (h % 2) + 1):
-                    emit(c, m, c * CH, CH, "s"[m % 1])
+            interleave(b, 0, CH - XG)
             quant_wave(h)
-            quant_basis(h + 3)
-            if h == 1:
-                mq(2)
-                mq(3)
+            if b + 1 < NB:
+                widen(b + 1, planes, "v")
 
-        h = NSTEP - 1
-        last = NCH - 1
-        halves = ((0, CH // 2), (CH // 2, CH))
-        for j, (n0, n1) in enumerate(halves):
-            for m in range(4):
-                if j == 0 or m < PH:
-                    mix_pass((last, j), m, h - 1, n0, n1, True, False, "mo" if j == 0 else "ph")
-        for n0, n1 in halves:
-            amplify(h, n0, n1)
-        emit(last - 1, 2, (last - 1) * CH, CH, "s")
-        emit(last - 1, 3, (last - 1) * CH, CH, "s")
-        for n0, n1 in halves:
-            quant_wave(h, n0, n1)
-        for j, (n0, n1) in enumerate(halves):
-            for m in range(4):
-                if j == 1 and m >= PH:
-                    mix_pass((last, j), m, h - 1, n0, n1, True, False)
-                mix_pass((last, j), m, h, n0, n1, False, True)
-            for m in range(4):
-                emit((last, j), m, last * CH + n0, n1 - n0, "vs"[m % 2])
+        sines(1)
+        widen(5, (2, 3), "s")
+        step(0, (0, 1))
+        quant_basis(4)
+        sines(2)
+        for c in range(4):
+            tm(c)
+        widen(6, (2, 3), "s")
+        step(1, (0, 1))
+        mq(0)
+        mq(1)
+        quant_basis(5)
+        sines(3)
+        widen(7, (3,), "s")
+        sines(4)
+        step(2, (0, 1, 2))
+        mq(2)
+        mq(3)
+        quant_basis(6)
+        out_rows(0, (0,), "s")
+        out_rows(0, (1,), "s")
+        sines(5)
+        out_rows(0, (2,), "s")
+        out_rows(0, (3,), "s")
+        step(3, ())
+        quant_basis(7)
+
+        out_rows(1, (0,), "s")
+        out_rows(1, (1,), "s")
+        mix_bank(1, (2,))
+        sines(6, (0, 1))
+        amplify_gp(4, VA, CH)
+        amplify(4, 0, VA)
+        emit(1, (2,), "v")
+        mix_bank(1, (3,))
+        sines(6, (2, 3))
+        quant_wave(4, 0, VA)
+        quant_wave(4, VA, CH)
+        amplify_gp(5, VA, CH)
+        amplify(5, 0, VA)
+        emit(1, (3,), "v")
+        sines(7)
+        quant_wave(5, 0, VA)
+        quant_wave(5, VA, CH)
+        amplify_gp(6, VA, CH)
+        amplify(6, 0, 256)
+        amplify(7, 0, 256)
+        for m in range(4):
+            out_rows(2, (m,), "s")
+        quant_wave(6, 0, 256)
+        amplify(6, 256, VA)
+        quant_wave(7, 0, 256)
+        quant_wave(6, VA, CH)
+        amplify(7, 256, VA)
+        quant_wave(6, 256, VA)
+        amplify(7, VA, CH)
+        out_rows(3, (0, 1), "s", 0, 256)
+        out_rows(3, (2, 3), "s", 0, 256)
+        quant_wave(7, 256, VA)
+        quant_wave(7, VA, CH)
+        out_rows(3, (0, 1, 2, 3), "s", 256, VA)
+        out_rows(3, (0, 1), "v", VA, CH, "ph")
+        out_rows(3, (2, 3), "s", VA, CH, "ph")

@@ -23,7 +23,7 @@ NB = 2 * NCH
 PH = 3
 SN = 4
 LEAD = 4
-XG = 288
+XG = 320
 VA = 384
 
 
@@ -44,7 +44,7 @@ def tile_additive_sine_synthesis_s7_kernel(
         on = keep.tile([PART, 2, 4], BF16, name="on")
         am_bf = keep.tile([PART, 2, 4], BF16, name="am_bf")
         am = psum.tile([PART, 2, 4], F32, name="am", tag="am", bufs=1)
-        raw = [[keep.tile([PART, 2, CH], U8, name="raw%d_%d" % (b, u)) for u in range(2)] for b in range(NB)]
+        raw = {}
         fx = [keep.tile([PART, K], BF16, name="fx%d" % i, align_bytes=64) for i in range(8)]
         mx = [keep.tile([PART, P], BF16, name="mx%d" % c, align_bytes=64) for c in range(4)]
         fc = keep.tile([PART, 8, 2 * PART], U32, name="fc", align_bytes=64)
@@ -59,10 +59,13 @@ def tile_additive_sine_synthesis_s7_kernel(
         mix_v = mix.rearrange("(c m) k -> c m k", m=PART)
         out_v = out.rearrange("(m p) n -> p m n", p=PART)
 
-        def load_basis(b):
+        def load_basis(b, planes=slice(0, 4)):
             c, g = b // 2, b % 2
-            for u in range(2):
-                nc.sync.dma_start(out=raw[b][u][:], in_=basis_v[g, :, 2 * u : 2 * u + 2, c * CH : (c + 1) * CH])
+            held = range(4)[planes]
+            piece = keep.tile([PART, len(held), CH], U8, name="raw%d_%d" % (b, held[0]))
+            nc.sync.dma_start(out=piece[:], in_=basis_v[g, :, planes, c * CH : (c + 1) * CH])
+            for j, t in enumerate(held):
+                raw[b, t] = piece[:, j, :]
 
         def load_freq(i):
             nc.sync.dma_start(out=fx[i][:], in_=freq_v[i // 4, i % 4])
@@ -86,7 +89,7 @@ def tile_additive_sine_synthesis_s7_kernel(
                 wid[b] = work.tile([PART, 4, CH], BF16, name="wid", tag="wid", align_bytes=64)
             g = b % 2
             for t in planes:
-                src = raw[b][t // 2][:, t % 2, :].bitcast(FP8)
+                src = raw[b, t].bitcast(FP8)
                 if engine == "v":
                     nc.vector.tensor_scalar(
                         out=wid[b][:, t, :], in0=src, scalar1=sc[:, g, t : t + 1], scalar2=None, op0=MULT
@@ -238,6 +241,19 @@ def tile_additive_sine_synthesis_s7_kernel(
                 mix_pass(yo[key][:, j, :], m, 2 * c, n0, n1, True, False)
                 mix_pass(yo[key][:, j, :], m, 2 * c + 1, n0, n1, False, True)
 
+        def mix_open(c, rows, n0, n1, tag="mo"):
+            key = (c, rows, n0)
+            if tag == "mo":
+                yo[key] = psum.tile([PART, len(rows), n1 - n0], F32, name="mo", tag="mo")
+            else:
+                yo[key] = psum.tile([PART, len(rows), n1 - n0], F32, name="ph", tag="ph", bufs=PH)
+            for j, m in enumerate(rows):
+                mix_pass(yo[key][:, j, :], m, 2 * c, n0, n1, j == 0, False)
+
+        def mix_close(c, rows, n0, n1):
+            for j, m in enumerate(rows):
+                mix_pass(yo[c, rows, n0][:, j, :], m, 2 * c + 1, n0, n1, False, j == len(rows) - 1)
+
         def emit(c, rows, engine, n0=0, n1=CH):
             res = work.tile([PART, len(rows), n1 - n0], F32, name="res", tag="res", bufs=8)
             if engine == "v":
@@ -251,12 +267,14 @@ def tile_additive_sine_synthesis_s7_kernel(
             emit(c, rows, engine, n0, n1)
 
         nc.scalar.dma_start(out=sc[:], in_=basis_scale.rearrange("(g p t) o -> p g (t o)", p=PART, t=4))
-        nc.scalar.dma_start(out=on[:], in_=onset.rearrange("(g p t) -> p g t", p=PART, t=4))
-        nc.scalar.dma_start(out=am_bf[:], in_=amp.rearrange("(g p t) -> p g t", p=PART, t=4))
         nc.gpsimd.memset(dummy[:], 0.0)
         make_identity(nc, ident[:])
         make_identity(nc, ident_bf[:])
         nc.scalar.activation(out=dummy[:], in_=dummy[:], func=ACTF.Sin)
+
+        def load_small():
+            nc.sync.dma_start(out=on[:], in_=onset.rearrange("(g p t) -> p g t", p=PART, t=4))
+            nc.sync.dma_start(out=am_bf[:], in_=amp.rearrange("(g p t) -> p g t", p=PART, t=4))
 
         def amp_to_psum():
             nc.tensor.matmul(
@@ -267,11 +285,17 @@ def tile_additive_sine_synthesis_s7_kernel(
                 stop=True,
             )
 
-        load_basis(0)
-        load_basis(1)
+        load_basis(0, slice(0, 1))
+        load_basis(0, slice(2, 3))
+        load_basis(0, slice(1, 4, 2))
+        load_basis(1, slice(0, 2))
+        load_basis(1, slice(2, 4))
         load_basis(2)
-        for i in range(4):
-            load_freq(i)
+        load_freq(0)
+        load_freq(1)
+        load_small()
+        load_freq(2)
+        load_freq(3)
         load_basis(3)
         for i in range(4, 8):
             load_freq(i)
@@ -303,7 +327,6 @@ def tile_additive_sine_synthesis_s7_kernel(
         fq(2)
         interleave(2, 0, CH)
         fq(3)
-        quant_basis(2)
         widen(3, (2,), "s")
         sines(0, (0,))
         widen(3, (3,), "s")
@@ -313,17 +336,20 @@ def tile_additive_sine_synthesis_s7_kernel(
         sines(0, (3,))
         interleave(3, 0, CH)
         widen(4, (0, 1), "v")
+        quant_basis(2)
+        fq(4)
+        fq(5)
+        widen(4, (2,), "v")
+        fq(6)
+        fq(7)
+        widen(4, (3,), "v")
         quant_basis(3)
-        for i in range(4, 8):
-            fq(i)
-        widen(4, (2, 3), "v")
 
         def step(h, planes):
             b = h + LEAD
             interleave_gp(b, CH - XG, CH)
             amplify(h)
             interleave(b, 0, CH - XG)
-            quant_wave(h)
             if b + 1 < NB:
                 widen(b + 1, planes, "v")
 
@@ -331,62 +357,72 @@ def tile_additive_sine_synthesis_s7_kernel(
         widen(5, (2, 3), "s")
         step(0, (0, 1))
         quant_basis(4)
+        quant_wave(0)
         sines(2)
         for c in range(4):
             tm(c)
         widen(6, (2, 3), "s")
         step(1, (0, 1))
-        mq(0)
-        mq(1)
+        for c in range(4):
+            mq(c)
         quant_basis(5)
+        quant_wave(1)
         sines(3)
-        widen(7, (3,), "s")
-        sines(4)
-        step(2, (0, 1, 2))
-        mq(2)
-        mq(3)
+        widen(7, (1, 2, 3), "s")
+        sines(4, (0, 1))
+        mix_bank(0, (0,))
+        mix_bank(0, (1,))
+        sines(4, (2, 3))
+        mix_bank(0, (2,))
+        mix_bank(0, (3,))
+        step(2, (0,))
         quant_basis(6)
-        out_rows(0, (0,), "s")
-        out_rows(0, (1,), "s")
+        quant_wave(2)
+        emit(0, (0,), "s")
+        emit(0, (1,), "s")
         sines(5)
-        out_rows(0, (2,), "s")
-        out_rows(0, (3,), "s")
         step(3, ())
+        quant_wave(3)
         quant_basis(7)
 
         out_rows(1, (0,), "s")
         out_rows(1, (1,), "s")
-        mix_bank(1, (2,))
-        sines(6, (0, 1))
+        sines(6)
+        sines(7)
         amplify_gp(4, VA, CH)
         amplify(4, 0, VA)
-        emit(1, (2,), "v")
-        mix_bank(1, (3,))
-        sines(6, (2, 3))
-        quant_wave(4, 0, VA)
+        emit(0, (2,), "v")
         quant_wave(4, VA, CH)
+        quant_wave(4, 0, VA)
         amplify_gp(5, VA, CH)
         amplify(5, 0, VA)
-        emit(1, (3,), "v")
-        sines(7)
-        quant_wave(5, 0, VA)
+        emit(0, (3,), "v")
+        out_rows(1, (2,), "s")
+        out_rows(1, (3,), "s")
         quant_wave(5, VA, CH)
+        quant_wave(5, 0, VA)
+        for m in range(4):
+            out_rows(2, (m,), "s")
         amplify_gp(6, VA, CH)
         amplify(6, 0, 256)
         amplify(7, 0, 256)
-        for m in range(4):
-            out_rows(2, (m,), "s")
         quant_wave(6, 0, 256)
-        amplify(6, 256, VA)
-        quant_wave(7, 0, 256)
         quant_wave(6, VA, CH)
-        amplify(7, 256, VA)
-        quant_wave(6, 256, VA)
-        amplify(7, VA, CH)
+        quant_wave(7, 0, 256)
         out_rows(3, (0, 1), "s", 0, 256)
         out_rows(3, (2, 3), "s", 0, 256)
+        mix_open(3, (0, 1), VA, CH, "ph")
+        mix_open(3, (2, 3), VA, CH, "ph")
+        amplify(6, 256, VA)
+        amplify(7, 256, VA)
+        quant_wave(6, 256, VA)
+        mix_open(3, (0, 1, 2, 3), 256, VA, "ph")
         quant_wave(7, 256, VA)
+        mix_close(3, (0, 1, 2, 3), 256, VA)
+        emit(3, (0, 1, 2, 3), "s", 256, VA)
+        amplify(7, VA, CH)
         quant_wave(7, VA, CH)
-        out_rows(3, (0, 1, 2, 3), "s", 256, VA)
-        out_rows(3, (0, 1), "v", VA, CH, "ph")
-        out_rows(3, (2, 3), "s", VA, CH, "ph")
+        mix_close(3, (0, 1), VA, CH)
+        mix_close(3, (2, 3), VA, CH)
+        emit(3, (0, 1), "v", VA, CH)
+        emit(3, (2, 3), "s", VA, CH)

@@ -267,14 +267,12 @@ def tile_additive_sine_synthesis_s7_kernel(
             emit(c, rows, engine, n0, n1)
 
         nc.scalar.dma_start(out=sc[:], in_=basis_scale.rearrange("(g p t) o -> p g (t o)", p=PART, t=4))
+        nc.scalar.dma_start(out=on[:], in_=onset.rearrange("(g p t) -> p g t", p=PART, t=4))
+        nc.scalar.dma_start(out=am_bf[:], in_=amp.rearrange("(g p t) -> p g t", p=PART, t=4))
         nc.gpsimd.memset(dummy[:], 0.0)
         make_identity(nc, ident[:])
         make_identity(nc, ident_bf[:])
         nc.scalar.activation(out=dummy[:], in_=dummy[:], func=ACTF.Sin)
-
-        def load_small():
-            nc.sync.dma_start(out=on[:], in_=onset.rearrange("(g p t) -> p g t", p=PART, t=4))
-            nc.sync.dma_start(out=am_bf[:], in_=amp.rearrange("(g p t) -> p g t", p=PART, t=4))
 
         def amp_to_psum():
             nc.tensor.matmul(
@@ -288,12 +286,10 @@ def tile_additive_sine_synthesis_s7_kernel(
         load_basis(0, slice(0, 1))
         load_basis(0, slice(2, 3))
         load_basis(0, slice(1, 4, 2))
-        load_basis(1, slice(0, 2))
-        load_basis(1, slice(2, 4))
+        load_basis(1)
         load_basis(2)
         load_freq(0)
         load_freq(1)
-        load_small()
         load_freq(2)
         load_freq(3)
         load_basis(3)

@@ -20,10 +20,9 @@ PART = 128
 CH = 512
 NCH = T // CH
 NB = 2 * NCH
-PH = 3
 SN = 4
 LEAD = 4
-XG = 320
+XG = 352
 VA = 384
 
 
@@ -34,7 +33,7 @@ def tile_additive_sine_synthesis_s7_kernel(
     with ExitStack() as ctx:
         keep = ctx.enter_context(tc.tile_pool(name="keep", bufs=1))
         work = ctx.enter_context(tc.tile_pool(name="work", bufs=3))
-        psum = ctx.enter_context(tc.psum_pool(name="psum", bufs=4))
+        psum = ctx.enter_context(tc.psum_pool(name="psum", bufs=1))
         ctx.enter_context(tc.manual_schedule())
 
         ident = keep.tile([PART, PART], F32, name="ident")
@@ -43,7 +42,7 @@ def tile_additive_sine_synthesis_s7_kernel(
         sc = keep.tile([PART, 2, 4], F32, name="sc")
         on = keep.tile([PART, 2, 4], BF16, name="on")
         am_bf = keep.tile([PART, 2, 4], BF16, name="am_bf")
-        am = psum.tile([PART, 2, 4], F32, name="am", tag="am", bufs=1)
+        am = psum.tile([PART, 2, 4], F32, name="am", tag="am")
         raw = {}
         fx = [keep.tile([PART, K], BF16, name="fx%d" % i, align_bytes=64) for i in range(8)]
         mx = [keep.tile([PART, P], BF16, name="mx%d" % c, align_bytes=64) for c in range(4)]
@@ -129,51 +128,65 @@ def tile_additive_sine_synthesis_s7_kernel(
                 in_=inter[b][:, n0:n1, :].rearrange("p n t -> p (n t)"),
             )
 
-        def turn(key, rows):
-            words = rows.bitcast(F32)
-            tr[key] = psum.tile([PART, 2, 2, PART], F32, name="mo", tag="mo")
-            for g in range(2):
-                for u in range(2):
-                    nc.tensor.transpose(
-                        tr[key][:, g, u, :], words[:, 256 * g + u : 256 * (g + 1) : 2], ident[:]
-                    )
+        free_banks = list(range(7))
+        bank_of = {}
 
-        def turn_out(key, engine="s"):
-            grouped[key] = work.tile([PART, 2, PART, 4], BF16, name="grouped", tag="grouped", align_bytes=64, bufs=4)
-            dst = grouped[key][:].rearrange("p g r t -> p (g r t)").bitcast(F32).rearrange(
-                "p (g r u) -> p g r u", g=2, u=2
-            )
-            src = tr[key][:].rearrange("p g u r -> p g r u")
-            if engine == "s":
-                nc.scalar.copy(out=dst, in_=src)
-            else:
-                nc.vector.tensor_copy(out=dst, in_=src)
+        def take_bank(key, shape):
+            bank_of[key] = free_banks.pop(0)
+            return psum.tile(shape, F32, name="bank", tag="bank%d" % bank_of[key])
 
-        def turn_quant(key, codes, scales):
+        def give_bank(key):
+            free_banks.append(bank_of[key])
+
+        def last_first(items):
+            return items[-1:] + items[:-1]
+
+        def turn(name, rows, tiles, codes, scales):
+            staged = work.tile([PART, len(tiles), 2, PART, 4], BF16, name="staged", tag="staged", align_bytes=64)
+            for i in tiles:
+                words = rows[i][:].bitcast(F32)
+                tr[name, i] = take_bank((name, i), [PART, 2, 2, PART])
+                for g in range(2):
+                    for u in range(2):
+                        nc.tensor.transpose(
+                            tr[name, i][:, g, u, :], words[:, 256 * g + u : 256 * (g + 1) : 2], ident[:]
+                        )
+            for i in last_first(tiles):
+                dst = staged[:, i - tiles[0]].rearrange("p g r t -> p (g r t)").bitcast(F32)
+                nc.scalar.copy(
+                    out=dst.rearrange("p (g r u) -> p g r u", g=2, u=2),
+                    in_=tr[name, i][:].rearrange("p g u r -> p g r u"),
+                )
+                give_bank((name, i))
+            grouped[name, tiles[0]] = (staged, tiles, codes, scales)
+
+        def turn_quant(name, first):
+            staged, tiles, codes, scales = grouped[name, first]
+            span = slice(tiles[0], tiles[-1] + 1)
             nc.vector.quantize_mx(
-                out=codes.bitcast(FP8X4), scales=scales, in_=grouped[key][:].rearrange("p g r t -> p (g r t)")
+                out=codes[:, span, :].rearrange("p i c -> p (i c)").bitcast(FP8X4),
+                scales=scales[:, span, :].rearrange("p i c -> p (i c)"),
+                in_=staged[:].rearrange("p i g r t -> p (i g r t)"),
             )
 
-        def tf(i, engine="s"):
-            turn(("f", i), fx[i][:])
-            turn_out(("f", i), engine)
+        def tf(*tiles):
+            turn("f", fx, tiles, fc, fs)
 
-        def tm(c, engine="s"):
-            turn(("m", c), mx[c][:])
-            turn_out(("m", c), engine)
+        def tm(*tiles):
+            turn("m", mx, tiles, mc, ms)
 
         def fq(i):
-            turn_quant(("f", i), fc[:, i, :], fs[:, i, :])
+            turn_quant("f", i)
 
         def mq(c):
-            turn_quant(("m", c), mc[:, c, :], ms[:, c, :])
+            turn_quant("m", c)
 
-        def sines(h, planes=range(4)):
+        def sines(h, planes=(0, 1, 2, 3)):
             c, half = h // 2, h % 2
             if h not in sn:
                 sn[h] = work.tile([PART, 4, CH], F32, name="sn", tag="sn", bufs=SN)
             for t in planes:
-                ph[h, t] = psum.tile([PART, CH], F32, name="ph", tag="ph", bufs=PH)
+                ph[h, t] = take_bank(("ph", h, t), [PART, CH])
                 i = 4 * half + t
                 for g in range(2):
                     nc.tensor.matmul_mx(
@@ -185,9 +198,11 @@ def tile_additive_sine_synthesis_s7_kernel(
                         start=(g == 0),
                         stop=(g == 1),
                     )
+            for t in last_first(planes):
                 nc.scalar.activation(
                     out=sn[h][:, t, :], in_=ph[h, t][:], func=ACTF.Sin, bias=on[:, half, t : t + 1]
                 )
+                give_bank(("ph", h, t))
 
         def amplify(h, n0=0, n1=CH):
             w = n1 - n0
@@ -231,22 +246,16 @@ def tile_additive_sine_synthesis_s7_kernel(
                 stop=stop,
             )
 
-        def mix_bank(c, rows, n0=0, n1=CH, tag="mo"):
+        def mix_bank(c, rows, n0=0, n1=CH):
             key = (c, rows, n0)
-            if tag == "mo":
-                yo[key] = psum.tile([PART, len(rows), n1 - n0], F32, name="mo", tag="mo")
-            else:
-                yo[key] = psum.tile([PART, len(rows), n1 - n0], F32, name="ph", tag="ph", bufs=PH)
+            yo[key] = take_bank(key, [PART, len(rows), n1 - n0])
             for j, m in enumerate(rows):
                 mix_pass(yo[key][:, j, :], m, 2 * c, n0, n1, True, False)
                 mix_pass(yo[key][:, j, :], m, 2 * c + 1, n0, n1, False, True)
 
-        def mix_open(c, rows, n0, n1, tag="mo"):
+        def mix_open(c, rows, n0, n1):
             key = (c, rows, n0)
-            if tag == "mo":
-                yo[key] = psum.tile([PART, len(rows), n1 - n0], F32, name="mo", tag="mo")
-            else:
-                yo[key] = psum.tile([PART, len(rows), n1 - n0], F32, name="ph", tag="ph", bufs=PH)
+            yo[key] = take_bank(key, [PART, len(rows), n1 - n0])
             for j, m in enumerate(rows):
                 mix_pass(yo[key][:, j, :], m, 2 * c, n0, n1, j == 0, False)
 
@@ -255,24 +264,31 @@ def tile_additive_sine_synthesis_s7_kernel(
                 mix_pass(yo[c, rows, n0][:, j, :], m, 2 * c + 1, n0, n1, False, j == len(rows) - 1)
 
         def emit(c, rows, engine, n0=0, n1=CH):
-            res = work.tile([PART, len(rows), n1 - n0], F32, name="res", tag="res", bufs=8)
+            res = keep.tile([PART, len(rows), n1 - n0], F32, name="res%d_%d_%d" % (c, rows[0], n0))
             if engine == "v":
                 nc.vector.tensor_copy(out=res[:], in_=yo[c, rows, n0][:])
             else:
                 nc.scalar.copy(out=res[:], in_=yo[c, rows, n0][:])
+            give_bank((c, rows, n0))
             nc.sync.dma_start(out=out_v[:, rows[0] : rows[-1] + 1, c * CH + n0 : c * CH + n1], in_=res[:])
 
-        def out_rows(c, rows, engine, n0=0, n1=CH, tag="mo"):
-            mix_bank(c, rows, n0, n1, tag)
-            emit(c, rows, engine, n0, n1)
+        def outs(c, tiles):
+            for m in tiles:
+                mix_bank(c, (m,))
+            for m in last_first(tiles):
+                emit(c, (m,), "s")
 
         nc.scalar.dma_start(out=sc[:], in_=basis_scale.rearrange("(g p t) o -> p g (t o)", p=PART, t=4))
-        nc.scalar.dma_start(out=on[:], in_=onset.rearrange("(g p t) -> p g t", p=PART, t=4))
-        nc.scalar.dma_start(out=am_bf[:], in_=amp.rearrange("(g p t) -> p g t", p=PART, t=4))
         nc.gpsimd.memset(dummy[:], 0.0)
         make_identity(nc, ident[:])
         make_identity(nc, ident_bf[:])
         nc.scalar.activation(out=dummy[:], in_=dummy[:], func=ACTF.Sin)
+
+        def load_onset():
+            nc.sync.dma_start(out=on[:], in_=onset.rearrange("(g p t) -> p g t", p=PART, t=4))
+
+        def load_amp():
+            nc.sync.dma_start(out=am_bf[:], in_=amp.rearrange("(g p t) -> p g t", p=PART, t=4))
 
         def amp_to_psum():
             nc.tensor.matmul(
@@ -286,16 +302,19 @@ def tile_additive_sine_synthesis_s7_kernel(
         load_basis(0, slice(0, 1))
         load_basis(0, slice(2, 3))
         load_basis(0, slice(1, 4, 2))
-        load_basis(1)
+        load_basis(1, slice(0, 2))
+        load_basis(1, slice(2, 4))
         load_basis(2)
         load_freq(0)
         load_freq(1)
         load_freq(2)
+        load_onset()
         load_freq(3)
         load_basis(3)
         for i in range(4, 8):
             load_freq(i)
         load_basis(4)
+        load_amp()
         load_basis(5)
         for c in range(4):
             load_mix(c)
@@ -312,7 +331,6 @@ def tile_additive_sine_synthesis_s7_kernel(
         tf(1)
         tf(2)
         tf(3)
-        amp_to_psum()
         interleave(0, 0, CH)
         interleave(1, 0, CH)
         quant_basis(0)
@@ -326,10 +344,12 @@ def tile_additive_sine_synthesis_s7_kernel(
         widen(3, (2,), "s")
         sines(0, (0,))
         widen(3, (3,), "s")
-        sines(0, (1, 2))
+        sines(0, (1,))
+        sines(0, (2,))
         for i in range(4, 8):
             tf(i)
         sines(0, (3,))
+        amp_to_psum()
         interleave(3, 0, CH)
         widen(4, (0, 1), "v")
         quant_basis(2)
@@ -341,6 +361,10 @@ def tile_additive_sine_synthesis_s7_kernel(
         widen(4, (3,), "v")
         quant_basis(3)
 
+        def out_rows(c, rows, engine, n0=0, n1=CH):
+            mix_bank(c, rows, n0, n1)
+            emit(c, rows, engine, n0, n1)
+
         def step(h, planes):
             b = h + LEAD
             interleave_gp(b, CH - XG, CH)
@@ -349,26 +373,35 @@ def tile_additive_sine_synthesis_s7_kernel(
             if b + 1 < NB:
                 widen(b + 1, planes, "v")
 
-        sines(1)
+        for t in range(4):
+            sines(1, (t,))
         widen(5, (2, 3), "s")
         step(0, (0, 1))
         quant_basis(4)
         quant_wave(0)
-        sines(2)
-        for c in range(4):
-            tm(c)
-        widen(6, (2, 3), "s")
-        step(1, (0, 1))
+        sines(2, (0,))
+        sines(2, (1,))
+        tm(0)
+        tm(1)
+        sines(2, (2,))
+        sines(2, (3,))
+        tm(2)
+        tm(3)
+        widen(6, (1, 2, 3), "s")
+        step(1, (0,))
         for c in range(4):
             mq(c)
         quant_basis(5)
         quant_wave(1)
-        sines(3)
+        for t in range(4):
+            sines(3, (t,))
         widen(7, (1, 2, 3), "s")
-        sines(4, (0, 1))
+        sines(4, (0,))
+        sines(4, (1,))
         mix_bank(0, (0,))
         mix_bank(0, (1,))
-        sines(4, (2, 3))
+        sines(4, (2,))
+        sines(4, (3,))
         mix_bank(0, (2,))
         mix_bank(0, (3,))
         step(2, (0,))
@@ -376,24 +409,28 @@ def tile_additive_sine_synthesis_s7_kernel(
         quant_wave(2)
         emit(0, (0,), "s")
         emit(0, (1,), "s")
-        sines(5)
+        emit(0, (2,), "s")
+        for t in range(4):
+            sines(5, (t,))
         step(3, ())
         quant_wave(3)
         quant_basis(7)
 
         out_rows(1, (0,), "s")
         out_rows(1, (1,), "s")
-        sines(6)
-        sines(7)
+        for t in range(4):
+            sines(6, (t,))
+        mix_bank(1, (2,))
+        for t in range(4):
+            sines(7, (t,))
         amplify_gp(4, VA, CH)
         amplify(4, 0, VA)
-        emit(0, (2,), "v")
+        emit(0, (3,), "v")
         quant_wave(4, VA, CH)
         quant_wave(4, 0, VA)
         amplify_gp(5, VA, CH)
         amplify(5, 0, VA)
-        emit(0, (3,), "v")
-        out_rows(1, (2,), "s")
+        emit(1, (2,), "v")
         out_rows(1, (3,), "s")
         quant_wave(5, VA, CH)
         quant_wave(5, 0, VA)
@@ -407,12 +444,12 @@ def tile_additive_sine_synthesis_s7_kernel(
         quant_wave(7, 0, 256)
         out_rows(3, (0, 1), "s", 0, 256)
         out_rows(3, (2, 3), "s", 0, 256)
-        mix_open(3, (0, 1), VA, CH, "ph")
-        mix_open(3, (2, 3), VA, CH, "ph")
+        mix_open(3, (0, 1), VA, CH)
+        mix_open(3, (2, 3), VA, CH)
         amplify(6, 256, VA)
         amplify(7, 256, VA)
         quant_wave(6, 256, VA)
-        mix_open(3, (0, 1, 2, 3), 256, VA, "ph")
+        mix_open(3, (0, 1, 2, 3), 256, VA)
         quant_wave(7, 256, VA)
         mix_close(3, (0, 1, 2, 3), 256, VA)
         emit(3, (0, 1, 2, 3), "s", 256, VA)

@@ -22,7 +22,7 @@ NCH = T // CH
 NB = 2 * NCH
 SN = 4
 LEAD = 4
-XG = 352
+XG = 320
 VA = 384
 
 
@@ -350,9 +350,9 @@ def tile_additive_sine_synthesis_s7_kernel(
             tf(i)
         sines(0, (3,))
         amp_to_psum()
+        quant_basis(2)
         interleave(3, 0, CH)
         widen(4, (0, 1), "v")
-        quant_basis(2)
         fq(4)
         fq(5)
         widen(4, (2,), "v")
@@ -385,77 +385,84 @@ def tile_additive_sine_synthesis_s7_kernel(
         tm(1)
         sines(2, (2,))
         sines(2, (3,))
-        tm(2)
-        tm(3)
-        widen(6, (1, 2, 3), "s")
-        step(1, (0,))
-        for c in range(4):
-            mq(c)
+        widen(6, (2, 3), "s")
+        step(1, (0, 1))
+        mq(0)
+        mq(1)
         quant_basis(5)
         quant_wave(1)
         for t in range(4):
             sines(3, (t,))
-        widen(7, (1, 2, 3), "s")
+        tm(2)
+        tm(3)
+        widen(7, (3,), "s")
         sines(4, (0,))
         sines(4, (1,))
         mix_bank(0, (0,))
         mix_bank(0, (1,))
         sines(4, (2,))
         sines(4, (3,))
-        mix_bank(0, (2,))
-        mix_bank(0, (3,))
-        step(2, (0,))
+        step(2, (0, 1, 2))
+        mq(2)
+        mq(3)
         quant_basis(6)
         quant_wave(2)
         emit(0, (0,), "s")
         emit(0, (1,), "s")
-        emit(0, (2,), "s")
-        for t in range(4):
-            sines(5, (t,))
+        sines(5, (0,))
+        sines(5, (1,))
+        out_rows(0, (2,), "s")
+        sines(5, (2,))
+        sines(5, (3,))
+        out_rows(0, (3,), "s")
+        mix_open(1, (0,), 0, CH)
+        mix_open(1, (1,), 0, CH)
+        mix_open(1, (2,), 0, CH)
         step(3, ())
         quant_wave(3)
         quant_basis(7)
 
-        out_rows(1, (0,), "s")
-        out_rows(1, (1,), "s")
+        mix_close(1, (0,), 0, CH)
+        emit(1, (0,), "s")
+        mix_close(1, (1,), 0, CH)
         for t in range(4):
             sines(6, (t,))
-        mix_bank(1, (2,))
-        for t in range(4):
-            sines(7, (t,))
         amplify_gp(4, VA, CH)
         amplify(4, 0, VA)
-        emit(0, (3,), "v")
-        quant_wave(4, VA, CH)
+        emit(1, (1,), "v")
+        mix_close(1, (2,), 0, CH)
+        out_rows(1, (3,), "s")
+        for t in range(4):
+            sines(7, (t,))
         quant_wave(4, 0, VA)
+        quant_wave(4, VA, CH)
         amplify_gp(5, VA, CH)
         amplify(5, 0, VA)
         emit(1, (2,), "v")
-        out_rows(1, (3,), "s")
-        quant_wave(5, VA, CH)
         quant_wave(5, 0, VA)
+        quant_wave(5, VA, CH)
         for m in range(4):
             out_rows(2, (m,), "s")
         amplify_gp(6, VA, CH)
         amplify(6, 0, 256)
         amplify(7, 0, 256)
         quant_wave(6, 0, 256)
-        quant_wave(6, VA, CH)
         quant_wave(7, 0, 256)
+        quant_wave(6, VA, CH)
         out_rows(3, (0, 1), "s", 0, 256)
         out_rows(3, (2, 3), "s", 0, 256)
-        mix_open(3, (0, 1), VA, CH)
-        mix_open(3, (2, 3), VA, CH)
+        mix_open(3, (0, 1, 2, 3), VA, CH)
+        amplify(7, VA, CH)
         amplify(6, 256, VA)
+        quant_wave(7, VA, CH)
+        mix_close(3, (0, 1, 2, 3), VA, CH)
+        emit(3, (0, 1, 2, 3), "s", VA, CH)
         amplify(7, 256, VA)
         quant_wave(6, 256, VA)
-        mix_open(3, (0, 1, 2, 3), 256, VA)
+        mix_open(3, (0, 1), 256, VA)
+        mix_open(3, (2, 3), 256, VA)
         quant_wave(7, 256, VA)
-        mix_close(3, (0, 1, 2, 3), 256, VA)
-        emit(3, (0, 1, 2, 3), "s", 256, VA)
-        amplify(7, VA, CH)
-        quant_wave(7, VA, CH)
-        mix_close(3, (0, 1), VA, CH)
-        mix_close(3, (2, 3), VA, CH)
-        emit(3, (0, 1), "v", VA, CH)
-        emit(3, (2, 3), "s", VA, CH)
+        mix_close(3, (0, 1), 256, VA)
+        mix_close(3, (2, 3), 256, VA)
+        emit(3, (0, 1), "v", 256, VA)
+        emit(3, (2, 3), "s", 256, VA)

@@ -17,13 +17,19 @@ ADD = mybir.AluOpType.add
 ACTF = mybir.ActivationFunctionType
 
 PART = 128
+PLANES = range(4)
 CH = 512
-NCH = T // CH
-NB = 2 * NCH
-SN = 4
+HALVES = 2 * T // CH
+FREQ_TILES = P // PART
+MIX_TILES = C // PART
+RING_BANKS = 7
 LEAD = 4
-XG = 320
-VA = 384
+SINE_BUFS = 4
+GP_COLS = 320
+AMP_SPLIT = 384
+GP_AMP_HALVES = (4, 5, 6)
+TAIL_SPLIT = 256
+VECTOR, SCALAR = "vector", "scalar"
 
 
 def tile_additive_sine_synthesis_s7_kernel(
@@ -38,97 +44,36 @@ def tile_additive_sine_synthesis_s7_kernel(
 
         ident = keep.tile([PART, PART], F32, name="ident")
         ident_bf = keep.tile([PART, PART], BF16, name="ident_bf")
-        dummy = keep.tile([PART, 1], F32, name="dummy")
-        sc = keep.tile([PART, 2, 4], F32, name="sc")
-        on = keep.tile([PART, 2, 4], BF16, name="on")
-        am_bf = keep.tile([PART, 2, 4], BF16, name="am_bf")
-        am = psum.tile([PART, 2, 4], F32, name="am", tag="am")
-        raw = {}
-        fx = [keep.tile([PART, K], BF16, name="fx%d" % i, align_bytes=64) for i in range(8)]
-        mx = [keep.tile([PART, P], BF16, name="mx%d" % c, align_bytes=64) for c in range(4)]
-        fc = keep.tile([PART, 8, 2 * PART], U32, name="fc", align_bytes=64)
-        fs = keep.tile([PART, 8, 2 * PART], U8, name="fs", align_bytes=64)
-        mc = keep.tile([PART, 4, 2 * PART], U32, name="mc", align_bytes=64)
-        ms = keep.tile([PART, 4, 2 * PART], U8, name="ms", align_bytes=64)
-        bc = keep.tile([PART, NB, CH], U32, name="bc", align_bytes=64)
-        bs = keep.tile([PART, NB, CH], U8, name="bs", align_bytes=64)
+        table_warm = keep.tile([PART, 1], F32, name="table_warm")
+        row_scale = keep.tile([PART, 2, 4], F32, name="row_scale")
+        onset_sb = keep.tile([PART, 2, 4], BF16, name="onset_sb")
+        amp_sb = keep.tile([PART, 2, 4], BF16, name="amp_sb")
+        amp_ps = psum.tile([PART, 2, 4], F32, name="amp_ps", tag="amp_ps")
+        freq_rows = [keep.tile([PART, K], BF16, name="freq_rows%d" % i, align_bytes=64) for i in range(FREQ_TILES)]
+        mix_rows = [keep.tile([PART, P], BF16, name="mix_rows%d" % m, align_bytes=64) for m in range(MIX_TILES)]
+        freq_codes = keep.tile([PART, FREQ_TILES, 2 * PART], U32, name="freq_codes", align_bytes=64)
+        freq_scales = keep.tile([PART, FREQ_TILES, 2 * PART], U8, name="freq_scales", align_bytes=64)
+        mix_codes = keep.tile([PART, MIX_TILES, 2 * PART], U32, name="mix_codes", align_bytes=64)
+        mix_scales = keep.tile([PART, MIX_TILES, 2 * PART], U8, name="mix_scales", align_bytes=64)
+        basis_codes = keep.tile([PART, HALVES, CH], U32, name="basis_codes", align_bytes=64)
+        basis_scales = keep.tile([PART, HALVES, CH], U8, name="basis_scales", align_bytes=64)
 
         basis_v = basis_bytes.rearrange("(g p t) n -> g p t n", p=PART, t=4)
-        freq_v = freq.rearrange("(h m t) k -> h t m k", m=PART, t=4)
-        mix_v = mix.rearrange("(c m) k -> c m k", m=PART)
+        freq_v = freq.rearrange("(g m t) k -> g t m k", m=PART, t=4)
+        mix_v = mix.rearrange("(i m) k -> i m k", m=PART)
         out_v = out.rearrange("(m p) n -> p m n", p=PART)
 
-        def load_basis(b, planes=slice(0, 4)):
-            c, g = b // 2, b % 2
-            held = range(4)[planes]
-            piece = keep.tile([PART, len(held), CH], U8, name="raw%d_%d" % (b, held[0]))
-            nc.sync.dma_start(out=piece[:], in_=basis_v[g, :, planes, c * CH : (c + 1) * CH])
-            for j, t in enumerate(held):
-                raw[b, t] = piece[:, j, :]
+        raw = {}
+        wide = {}
+        basis_in = {}
+        turned = {}
+        sine = {}
+        wave_in = {}
+        wave_codes = {}
+        wave_scales = {}
+        sums = {}
 
-        def load_freq(i):
-            nc.sync.dma_start(out=fx[i][:], in_=freq_v[i // 4, i % 4])
-
-        def load_mix(c):
-            nc.sync.dma_start(out=mx[c][:], in_=mix_v[c])
-
-        wid = {}
-        inter = {}
-        tr = {}
-        grouped = {}
-        ph = {}
-        sn = {}
-        wb = {}
-        wc = {}
-        ws = {}
-        yo = {}
-
-        def widen(b, planes, engine):
-            if b not in wid:
-                wid[b] = work.tile([PART, 4, CH], BF16, name="wid", tag="wid", align_bytes=64)
-            g = b % 2
-            for t in planes:
-                src = raw[b, t].bitcast(FP8)
-                if engine == "v":
-                    nc.vector.tensor_scalar(
-                        out=wid[b][:, t, :], in0=src, scalar1=sc[:, g, t : t + 1], scalar2=None, op0=MULT
-                    )
-                else:
-                    nc.scalar.activation(out=wid[b][:, t, :], in_=src, func=ACTF.Copy, scale=sc[:, g, t : t + 1])
-
-        def new_inter(b):
-            if b < LEAD:
-                return work.tile([PART, CH, 4], BF16, name="inter", tag="inter", align_bytes=64, bufs=2)
-            return work.tile([PART, CH, 4], BF16, name="shared", tag="shared", align_bytes=64, bufs=1)
-
-        def interleave(b, n0, n1):
-            if b not in inter:
-                inter[b] = new_inter(b)
-            nc.vector.tensor_copy(
-                out=inter[b][:, n0:n1, :].rearrange("p (c i) t -> p c t i", i=4),
-                in_=wid[b][:, :, n0:n1].rearrange("p t (c i) -> p c t i", i=4),
-            )
-
-        def interleave_gp(b, n0, n1):
-            if b not in inter:
-                inter[b] = new_inter(b)
-            nc.gpsimd.tensor_scalar(
-                out=inter[b][:, n0:n1, :],
-                in0=wid[b][:, :, n0:n1].rearrange("p t n -> p n t"),
-                scalar1=1.0,
-                scalar2=0.0,
-                op0=MULT,
-                op1=ADD,
-            )
-
-        def quant_basis(b, n0=0, n1=CH):
-            nc.vector.quantize_mx(
-                out=bc[:, b, n0:n1].bitcast(FP8X4),
-                scales=bs[:, b, n0:n1],
-                in_=inter[b][:, n0:n1, :].rearrange("p n t -> p (n t)"),
-            )
-
-        free_banks = list(range(7))
+        free_banks = list(range(RING_BANKS))
         bank_of = {}
 
         def take_bank(key, shape):
@@ -138,166 +83,217 @@ def tile_additive_sine_synthesis_s7_kernel(
         def give_bank(key):
             free_banks.append(bank_of[key])
 
-        def last_first(items):
-            return items[-1:] + items[:-1]
+        def load_basis(b, planes=slice(0, 4)):
+            c, g = b // 2, b % 2
+            held = PLANES[planes]
+            piece = keep.tile([PART, len(held), CH], U8, name="raw%d_%d" % (b, held[0]))
+            nc.sync.dma_start(out=piece[:], in_=basis_v[g, :, planes, c * CH : (c + 1) * CH])
+            for j, t in enumerate(held):
+                raw[b, t] = piece[:, j, :]
 
-        def turn(name, rows, tiles, codes, scales):
-            staged = work.tile([PART, len(tiles), 2, PART, 4], BF16, name="staged", tag="staged", align_bytes=64)
-            for i in tiles:
-                words = rows[i][:].bitcast(F32)
-                tr[name, i] = take_bank((name, i), [PART, 2, 2, PART])
-                for g in range(2):
-                    for u in range(2):
-                        nc.tensor.transpose(
-                            tr[name, i][:, g, u, :], words[:, 256 * g + u : 256 * (g + 1) : 2], ident[:]
-                        )
-            for i in last_first(tiles):
-                dst = staged[:, i - tiles[0]].rearrange("p g r t -> p (g r t)").bitcast(F32)
-                nc.scalar.copy(
-                    out=dst.rearrange("p (g r u) -> p g r u", g=2, u=2),
-                    in_=tr[name, i][:].rearrange("p g u r -> p g r u"),
-                )
-                give_bank((name, i))
-            grouped[name, tiles[0]] = (staged, tiles, codes, scales)
+        def load_freq(i):
+            nc.sync.dma_start(out=freq_rows[i][:], in_=freq_v[i // 4, i % 4])
 
-        def turn_quant(name, first):
-            staged, tiles, codes, scales = grouped[name, first]
-            span = slice(tiles[0], tiles[-1] + 1)
-            nc.vector.quantize_mx(
-                out=codes[:, span, :].rearrange("p i c -> p (i c)").bitcast(FP8X4),
-                scales=scales[:, span, :].rearrange("p i c -> p (i c)"),
-                in_=staged[:].rearrange("p i g r t -> p (i g r t)"),
+        def load_mix(m):
+            nc.sync.dma_start(out=mix_rows[m][:], in_=mix_v[m])
+
+        def load_by_plane(queue, dst, src):
+            queue.dma_start(out=dst[:], in_=src)
+
+        def widen(b, planes, engine):
+            if b not in wide:
+                wide[b] = work.tile([PART, 4, CH], BF16, name="wide", tag="wide", align_bytes=64)
+            for t in planes:
+                src = raw[b, t].bitcast(FP8)
+                factor = row_scale[:, b % 2, t : t + 1]
+                if engine == VECTOR:
+                    nc.vector.tensor_scalar(out=wide[b][:, t, :], in0=src, scalar1=factor, scalar2=None, op0=MULT)
+                else:
+                    nc.scalar.activation(out=wide[b][:, t, :], in_=src, func=ACTF.Copy, scale=factor)
+
+        def interleave(b, n1):
+            if b < LEAD:
+                basis_in[b] = work.tile([PART, CH, 4], BF16, name="basis_in", tag="basis_in", align_bytes=64, bufs=2)
+            nc.vector.tensor_copy(
+                out=basis_in[b][:, 0:n1, :].rearrange("p (c i) t -> p c t i", i=4),
+                in_=wide[b][:, :, 0:n1].rearrange("p t (c i) -> p c t i", i=4),
             )
 
-        def tf(*tiles):
-            turn("f", fx, tiles, fc, fs)
+        def interleave_gpsimd(b, n0):
+            basis_in[b] = work.tile([PART, CH, 4], BF16, name="basis_gp", tag="basis_gp", align_bytes=64, bufs=1)
+            nc.gpsimd.tensor_scalar(
+                out=basis_in[b][:, n0:CH, :],
+                in0=wide[b][:, :, n0:CH].rearrange("p t n -> p n t"),
+                scalar1=1.0,
+                scalar2=0.0,
+                op0=MULT,
+                op1=ADD,
+            )
 
-        def tm(*tiles):
-            turn("m", mx, tiles, mc, ms)
+        def quant_basis(b):
+            nc.vector.quantize_mx(
+                out=basis_codes[:, b, :].bitcast(FP8X4),
+                scales=basis_scales[:, b, :],
+                in_=basis_in[b][:].rearrange("p n t -> p (n t)"),
+            )
 
-        def fq(i):
-            turn_quant("f", i)
+        def turn(operand, rows, i):
+            turned[operand, i] = work.tile([PART, 2, PART, 4], BF16, name="turned", tag="turned", align_bytes=64)
+            words = rows[i][:].bitcast(F32)
+            bank = take_bank((operand, i), [PART, 2, 2, PART])
+            for g in range(2):
+                for u in range(2):
+                    nc.tensor.transpose(bank[:, g, u, :], words[:, 256 * g + u : 256 * (g + 1) : 2], ident[:])
+            dst = turned[operand, i][:].rearrange("p g r t -> p (g r t)").bitcast(F32)
+            nc.scalar.copy(
+                out=dst.rearrange("p (g r u) -> p g r u", g=2, u=2),
+                in_=bank[:].rearrange("p g u r -> p g r u"),
+            )
+            give_bank((operand, i))
 
-        def mq(c):
-            turn_quant("m", c)
+        def quant_turned(operand, codes, scales, i):
+            nc.vector.quantize_mx(
+                out=codes[:, i, :].bitcast(FP8X4),
+                scales=scales[:, i, :],
+                in_=turned[operand, i][:].rearrange("p g r t -> p (g r t)"),
+            )
 
-        def sines(h, planes=(0, 1, 2, 3)):
+        def turn_freq(i):
+            turn("freq", freq_rows, i)
+
+        def turn_mix(m):
+            turn("mix", mix_rows, m)
+
+        def quant_freq(i):
+            quant_turned("freq", freq_codes, freq_scales, i)
+
+        def quant_mix(m):
+            quant_turned("mix", mix_codes, mix_scales, m)
+
+        def sines(h, planes):
             c, half = h // 2, h % 2
-            if h not in sn:
-                sn[h] = work.tile([PART, 4, CH], F32, name="sn", tag="sn", bufs=SN)
+            if h not in sine:
+                sine[h] = work.tile([PART, 4, CH], F32, name="sine", tag="sine", bufs=SINE_BUFS)
             for t in planes:
-                ph[h, t] = take_bank(("ph", h, t), [PART, CH])
+                bank = take_bank(("phase", h, t), [PART, CH])
                 i = 4 * half + t
                 for g in range(2):
                     nc.tensor.matmul_mx(
-                        out=ph[h, t][:],
-                        lhsT=fc[:, i, PART * g : PART * (g + 1)].bitcast(FP8X4),
-                        lhsT_scale=fs[:, i, PART * g : PART * (g + 1)],
-                        rhs=bc[:, 2 * c + g, :].bitcast(FP8X4),
-                        rhs_scale=bs[:, 2 * c + g, :],
+                        out=bank[:],
+                        lhsT=freq_codes[:, i, PART * g : PART * (g + 1)].bitcast(FP8X4),
+                        lhsT_scale=freq_scales[:, i, PART * g : PART * (g + 1)],
+                        rhs=basis_codes[:, 2 * c + g, :].bitcast(FP8X4),
+                        rhs_scale=basis_scales[:, 2 * c + g, :],
                         start=(g == 0),
                         stop=(g == 1),
                     )
-            for t in last_first(planes):
                 nc.scalar.activation(
-                    out=sn[h][:, t, :], in_=ph[h, t][:], func=ACTF.Sin, bias=on[:, half, t : t + 1]
+                    out=sine[h][:, t, :], in_=bank[:], func=ACTF.Sin, bias=onset_sb[:, half, t : t + 1]
                 )
-                give_bank(("ph", h, t))
+                give_bank(("phase", h, t))
 
-        def amplify(h, n0=0, n1=CH):
-            w = n1 - n0
-            wb[h, n0] = work.tile([PART, w, 4], BF16, name="wb", tag="wb", align_bytes=64, bufs=4)
+        def relay_tile(h, width):
+            return work.tile([PART, width, 4], BF16, name="relay", tag="relay%d" % h, align_bytes=64, bufs=1)
+
+        def amplify(h, n0, n1):
+            width = n1 - n0
+            if h + 1 in GP_AMP_HALVES:
+                wave_in[h, n0] = relay_tile(h + 1, width)
+            else:
+                wave_in[h, n0] = work.tile(
+                    [PART, width, 4], BF16, name="wave_in", tag="wave_in", align_bytes=64, bufs=4
+                )
+            factor = amp_ps[:, h % 2, :].rearrange("p (c t i) -> p c t i", c=1, i=1)
             nc.vector.tensor_tensor(
-                out=wb[h, n0][:].rearrange("p (c i) t -> p c t i", i=4),
-                in0=sn[h][:, :, n0:n1].rearrange("p t (c i) -> p c t i", i=4),
-                in1=am[:, h % 2, :].rearrange("p (c t i) -> p c t i", c=1, i=1).to_broadcast([PART, w // 4, 4, 4]),
+                out=wave_in[h, n0][:].rearrange("p (c i) t -> p c t i", i=4),
+                in0=sine[h][:, :, n0:n1].rearrange("p t (c i) -> p c t i", i=4),
+                in1=factor.to_broadcast([PART, width // 4, 4, 4]),
                 op=MULT,
             )
 
-        def amplify_gp(h, n0, n1):
-            w = n1 - n0
-            wb[h, n0] = work.tile([PART, w, 4], BF16, name="shared", tag="shared", align_bytes=64, bufs=1)
+        def amplify_gpsimd(h):
+            width = CH - AMP_SPLIT
+            wave_in[h, AMP_SPLIT] = relay_tile(h, width)
+            factor = amp_sb[:, h % 2, :].rearrange("p (n t) -> p n t", n=1)
             nc.gpsimd.tensor_tensor(
-                out=wb[h, n0][:],
-                in0=sn[h][:, :, n0:n1].rearrange("p t n -> p n t"),
-                in1=am_bf[:, h % 2, :].rearrange("p (n t) -> p n t", n=1).to_broadcast([PART, w, 4]),
+                out=wave_in[h, AMP_SPLIT][:],
+                in0=sine[h][:, :, AMP_SPLIT:CH].rearrange("p t n -> p n t"),
+                in1=factor.to_broadcast([PART, width, 4]),
                 op=MULT,
             )
 
-        def quant_wave(h, n0=0, n1=CH):
-            if h not in wc:
-                wc[h] = work.tile([PART, CH], U32, name="wc", tag="wc", align_bytes=64, bufs=4)
-                ws[h] = work.tile([PART, CH], U8, name="ws", tag="ws", align_bytes=64, bufs=4)
+        def quant_wave(h, n0, n1):
+            if h not in wave_codes:
+                wave_codes[h] = work.tile([PART, CH], U32, name="wave_codes", tag="wave_codes", align_bytes=64, bufs=4)
+                wave_scales[h] = work.tile(
+                    [PART, CH], U8, name="wave_scales", tag="wave_scales", align_bytes=64, bufs=4
+                )
             nc.vector.quantize_mx(
-                out=wc[h][:, n0:n1].bitcast(FP8X4),
-                scales=ws[h][:, n0:n1],
-                in_=wb[h, n0][:].rearrange("p n t -> p (n t)"),
+                out=wave_codes[h][:, n0:n1].bitcast(FP8X4),
+                scales=wave_scales[h][:, n0:n1],
+                in_=wave_in[h, n0][:].rearrange("p n t -> p (n t)"),
             )
 
         def mix_pass(dst, m, h, n0, n1, start, stop):
-            half = h % 2
+            g = h % 2
             nc.tensor.matmul_mx(
                 out=dst,
-                lhsT=mc[:, m, PART * half : PART * (half + 1)].bitcast(FP8X4),
-                lhsT_scale=ms[:, m, PART * half : PART * (half + 1)],
-                rhs=wc[h][:, n0:n1].bitcast(FP8X4),
-                rhs_scale=ws[h][:, n0:n1],
+                lhsT=mix_codes[:, m, PART * g : PART * (g + 1)].bitcast(FP8X4),
+                lhsT_scale=mix_scales[:, m, PART * g : PART * (g + 1)],
+                rhs=wave_codes[h][:, n0:n1].bitcast(FP8X4),
+                rhs_scale=wave_scales[h][:, n0:n1],
                 start=start,
                 stop=stop,
             )
 
-        def mix_bank(c, rows, n0=0, n1=CH):
-            key = (c, rows, n0)
-            yo[key] = take_bank(key, [PART, len(rows), n1 - n0])
-            for j, m in enumerate(rows):
-                mix_pass(yo[key][:, j, :], m, 2 * c, n0, n1, True, False)
-                mix_pass(yo[key][:, j, :], m, 2 * c + 1, n0, n1, False, True)
+        def mix_bank(c, tiles, n0, n1):
+            key = (c, tiles, n0)
+            sums[key] = take_bank(key, [PART, len(tiles), n1 - n0])
+            for j, m in enumerate(tiles):
+                mix_pass(sums[key][:, j, :], m, 2 * c, n0, n1, True, False)
+                mix_pass(sums[key][:, j, :], m, 2 * c + 1, n0, n1, False, True)
 
-        def mix_open(c, rows, n0, n1):
-            key = (c, rows, n0)
-            yo[key] = take_bank(key, [PART, len(rows), n1 - n0])
-            for j, m in enumerate(rows):
-                mix_pass(yo[key][:, j, :], m, 2 * c, n0, n1, j == 0, False)
+        def mix_open(c, tiles, n0, n1):
+            key = (c, tiles, n0)
+            sums[key] = take_bank(key, [PART, len(tiles), n1 - n0])
+            for j, m in enumerate(tiles):
+                mix_pass(sums[key][:, j, :], m, 2 * c, n0, n1, j == 0, False)
 
-        def mix_close(c, rows, n0, n1):
-            for j, m in enumerate(rows):
-                mix_pass(yo[c, rows, n0][:, j, :], m, 2 * c + 1, n0, n1, False, j == len(rows) - 1)
+        def mix_close(c, tiles, n0, n1):
+            for j, m in enumerate(tiles):
+                mix_pass(sums[c, tiles, n0][:, j, :], m, 2 * c + 1, n0, n1, False, j == len(tiles) - 1)
 
-        def emit(c, rows, engine, n0=0, n1=CH):
-            res = keep.tile([PART, len(rows), n1 - n0], F32, name="res%d_%d_%d" % (c, rows[0], n0))
-            if engine == "v":
-                nc.vector.tensor_copy(out=res[:], in_=yo[c, rows, n0][:])
+        def store(c, tiles, n0, n1, engine):
+            res = keep.tile([PART, len(tiles), n1 - n0], F32, name="res%d_%d_%d" % (c, tiles[0], n0))
+            if engine == VECTOR:
+                nc.vector.tensor_copy(out=res[:], in_=sums[c, tiles, n0][:])
             else:
-                nc.scalar.copy(out=res[:], in_=yo[c, rows, n0][:])
-            give_bank((c, rows, n0))
-            nc.sync.dma_start(out=out_v[:, rows[0] : rows[-1] + 1, c * CH + n0 : c * CH + n1], in_=res[:])
+                nc.scalar.copy(out=res[:], in_=sums[c, tiles, n0][:])
+            give_bank((c, tiles, n0))
+            nc.sync.dma_start(out=out_v[:, tiles[0] : tiles[-1] + 1, c * CH + n0 : c * CH + n1], in_=res[:])
 
-        def outs(c, tiles):
-            for m in tiles:
-                mix_bank(c, (m,))
-            for m in last_first(tiles):
-                emit(c, (m,), "s")
+        def mix_and_store(c, tiles, n0, n1):
+            mix_bank(c, tiles, n0, n1)
+            store(c, tiles, n0, n1, SCALAR)
 
-        nc.scalar.dma_start(out=sc[:], in_=basis_scale.rearrange("(g p t) o -> p g (t o)", p=PART, t=4))
-        nc.gpsimd.memset(dummy[:], 0.0)
+        def window_with_basis(h):
+            interleave_gpsimd(h + LEAD, CH - GP_COLS)
+            amplify(h, 0, CH)
+            interleave(h + LEAD, CH - GP_COLS)
+
+        def window_with_share(h):
+            amplify_gpsimd(h)
+            amplify(h, 0, AMP_SPLIT)
+
+        def quant_shared(h):
+            quant_wave(h, 0, AMP_SPLIT)
+            quant_wave(h, AMP_SPLIT, CH)
+
+        load_by_plane(nc.scalar, row_scale, basis_scale.rearrange("(g p t) o -> p g (t o)", p=PART, t=4))
+        nc.gpsimd.memset(table_warm[:], 0.0)
         make_identity(nc, ident[:])
         make_identity(nc, ident_bf[:])
-        nc.scalar.activation(out=dummy[:], in_=dummy[:], func=ACTF.Sin)
-
-        def load_onset():
-            nc.sync.dma_start(out=on[:], in_=onset.rearrange("(g p t) -> p g t", p=PART, t=4))
-
-        def load_amp():
-            nc.sync.dma_start(out=am_bf[:], in_=amp.rearrange("(g p t) -> p g t", p=PART, t=4))
-
-        def amp_to_psum():
-            nc.tensor.matmul(
-                am[:].rearrange("p g t -> p (g t)"),
-                lhsT=ident_bf[:],
-                rhs=am_bf[:].rearrange("p g t -> p (g t)"),
-                start=True,
-                stop=True,
-            )
+        nc.scalar.activation(out=table_warm[:], in_=table_warm[:], func=ACTF.Sin)
 
         load_basis(0, slice(0, 1))
         load_basis(0, slice(2, 3))
@@ -305,164 +301,148 @@ def tile_additive_sine_synthesis_s7_kernel(
         load_basis(1, slice(0, 2))
         load_basis(1, slice(2, 4))
         load_basis(2)
-        load_freq(0)
-        load_freq(1)
-        load_freq(2)
-        load_onset()
+        for i in range(3):
+            load_freq(i)
+        load_by_plane(nc.sync, onset_sb, onset.rearrange("(g p t) -> p g t", p=PART, t=4))
         load_freq(3)
         load_basis(3)
-        for i in range(4, 8):
+        for i in range(4, FREQ_TILES):
             load_freq(i)
         load_basis(4)
-        load_amp()
+        load_by_plane(nc.sync, amp_sb, amp.rearrange("(g p t) -> p g t", p=PART, t=4))
         load_basis(5)
-        for c in range(4):
-            load_mix(c)
+        for m in range(MIX_TILES):
+            load_mix(m)
         load_basis(6)
         load_basis(7)
 
-        widen(0, (0, 1), "v")
-        widen(0, (2, 3), "s")
-        widen(1, (0, 1, 2), "v")
-        widen(1, (3,), "s")
-        widen(2, (0, 1, 2), "s")
-        tf(0)
-        widen(2, (3,), "s")
-        tf(1)
-        tf(2)
-        tf(3)
-        interleave(0, 0, CH)
-        interleave(1, 0, CH)
+        widen(0, (0, 1), VECTOR)
+        widen(0, (2, 3), SCALAR)
+        widen(1, (0, 1, 2), VECTOR)
+        widen(1, (3,), SCALAR)
+        widen(2, (0, 1, 2), SCALAR)
+        turn_freq(0)
+        widen(2, (3,), SCALAR)
+        for i in range(1, 4):
+            turn_freq(i)
+        interleave(0, CH)
+        interleave(1, CH)
         quant_basis(0)
-        fq(0)
+        quant_freq(0)
         quant_basis(1)
-        fq(1)
-        widen(3, (0, 1), "v")
-        fq(2)
-        interleave(2, 0, CH)
-        fq(3)
-        widen(3, (2,), "s")
+        quant_freq(1)
+        widen(3, (0, 1), VECTOR)
+        quant_freq(2)
+        interleave(2, CH)
+        quant_freq(3)
+        widen(3, (2,), SCALAR)
         sines(0, (0,))
-        widen(3, (3,), "s")
-        sines(0, (1,))
-        sines(0, (2,))
-        for i in range(4, 8):
-            tf(i)
+        widen(3, (3,), SCALAR)
+        sines(0, (1, 2))
+        for i in range(4, FREQ_TILES):
+            turn_freq(i)
         sines(0, (3,))
-        amp_to_psum()
+        nc.tensor.matmul(
+            amp_ps[:].rearrange("p g t -> p (g t)"),
+            lhsT=ident_bf[:],
+            rhs=amp_sb[:].rearrange("p g t -> p (g t)"),
+            start=True,
+            stop=True,
+        )
         quant_basis(2)
-        interleave(3, 0, CH)
-        widen(4, (0, 1), "v")
-        fq(4)
-        fq(5)
-        widen(4, (2,), "v")
-        fq(6)
-        fq(7)
-        widen(4, (3,), "v")
+        interleave(3, CH)
+        widen(4, (0, 1), VECTOR)
+        quant_freq(4)
+        quant_freq(5)
+        widen(4, (2,), VECTOR)
+        quant_freq(6)
+        quant_freq(7)
+        widen(4, (3,), VECTOR)
         quant_basis(3)
 
-        def out_rows(c, rows, engine, n0=0, n1=CH):
-            mix_bank(c, rows, n0, n1)
-            emit(c, rows, engine, n0, n1)
-
-        def step(h, planes):
-            b = h + LEAD
-            interleave_gp(b, CH - XG, CH)
-            amplify(h)
-            interleave(b, 0, CH - XG)
-            if b + 1 < NB:
-                widen(b + 1, planes, "v")
-
-        for t in range(4):
-            sines(1, (t,))
-        widen(5, (2, 3), "s")
-        step(0, (0, 1))
+        sines(1, PLANES)
+        widen(5, (2, 3), SCALAR)
+        window_with_basis(0)
+        widen(5, (0, 1), VECTOR)
         quant_basis(4)
-        quant_wave(0)
-        sines(2, (0,))
-        sines(2, (1,))
-        tm(0)
-        tm(1)
-        sines(2, (2,))
-        sines(2, (3,))
-        widen(6, (2, 3), "s")
-        step(1, (0, 1))
-        mq(0)
-        mq(1)
+        quant_wave(0, 0, CH)
+
+        sines(2, (0, 1))
+        turn_mix(0)
+        turn_mix(1)
+        sines(2, (2, 3))
+        widen(6, (2, 3), SCALAR)
+        window_with_basis(1)
+        widen(6, (0, 1), VECTOR)
+        quant_mix(0)
+        quant_mix(1)
         quant_basis(5)
-        quant_wave(1)
-        for t in range(4):
-            sines(3, (t,))
-        tm(2)
-        tm(3)
-        widen(7, (3,), "s")
-        sines(4, (0,))
-        sines(4, (1,))
-        mix_bank(0, (0,))
-        mix_bank(0, (1,))
-        sines(4, (2,))
-        sines(4, (3,))
-        step(2, (0, 1, 2))
-        mq(2)
-        mq(3)
+        quant_wave(1, 0, CH)
+
+        sines(3, PLANES)
+        turn_mix(2)
+        turn_mix(3)
+        widen(7, (2, 3), SCALAR)
+        sines(4, (0, 1))
+        mix_bank(0, (0,), 0, CH)
+        mix_bank(0, (1,), 0, CH)
+        sines(4, (2, 3))
+        window_with_basis(2)
+        widen(7, (0, 1), VECTOR)
+        quant_mix(2)
+        quant_mix(3)
         quant_basis(6)
-        quant_wave(2)
-        emit(0, (0,), "s")
-        emit(0, (1,), "s")
-        sines(5, (0,))
-        sines(5, (1,))
-        out_rows(0, (2,), "s")
-        sines(5, (2,))
-        sines(5, (3,))
-        out_rows(0, (3,), "s")
-        mix_open(1, (0,), 0, CH)
-        mix_open(1, (1,), 0, CH)
-        mix_open(1, (2,), 0, CH)
-        step(3, ())
-        quant_wave(3)
+        quant_wave(2, 0, CH)
+
+        store(0, (0,), 0, CH, SCALAR)
+        store(0, (1,), 0, CH, SCALAR)
+        sines(5, (0, 1))
+        mix_and_store(0, (2,), 0, CH)
+        sines(5, (2, 3))
+        mix_and_store(0, (3,), 0, CH)
+        for m in range(MIX_TILES):
+            mix_open(1, (m,), 0, CH)
+        window_with_basis(3)
+        quant_wave(3, 0, CH)
         quant_basis(7)
 
         mix_close(1, (0,), 0, CH)
-        emit(1, (0,), "s")
+        store(1, (0,), 0, CH, SCALAR)
         mix_close(1, (1,), 0, CH)
-        for t in range(4):
-            sines(6, (t,))
-        amplify_gp(4, VA, CH)
-        amplify(4, 0, VA)
-        emit(1, (1,), "v")
+        sines(6, PLANES)
+        window_with_share(4)
+        store(1, (1,), 0, CH, VECTOR)
         mix_close(1, (2,), 0, CH)
-        out_rows(1, (3,), "s")
-        for t in range(4):
-            sines(7, (t,))
-        quant_wave(4, 0, VA)
-        quant_wave(4, VA, CH)
-        amplify_gp(5, VA, CH)
-        amplify(5, 0, VA)
-        emit(1, (2,), "v")
-        quant_wave(5, 0, VA)
-        quant_wave(5, VA, CH)
-        for m in range(4):
-            out_rows(2, (m,), "s")
-        amplify_gp(6, VA, CH)
-        amplify(6, 0, 256)
-        amplify(7, 0, 256)
-        quant_wave(6, 0, 256)
-        quant_wave(7, 0, 256)
-        quant_wave(6, VA, CH)
-        out_rows(3, (0, 1), "s", 0, 256)
-        out_rows(3, (2, 3), "s", 0, 256)
-        mix_open(3, (0, 1, 2, 3), VA, CH)
-        amplify(7, VA, CH)
-        amplify(6, 256, VA)
-        quant_wave(7, VA, CH)
-        mix_close(3, (0, 1, 2, 3), VA, CH)
-        emit(3, (0, 1, 2, 3), "s", VA, CH)
-        amplify(7, 256, VA)
-        quant_wave(6, 256, VA)
-        mix_open(3, (0, 1), 256, VA)
-        mix_open(3, (2, 3), 256, VA)
-        quant_wave(7, 256, VA)
-        mix_close(3, (0, 1), 256, VA)
-        mix_close(3, (2, 3), 256, VA)
-        emit(3, (0, 1), "v", 256, VA)
-        emit(3, (2, 3), "s", 256, VA)
+        mix_close(1, (3,), 0, CH)
+        store(1, (3,), 0, CH, SCALAR)
+        sines(7, PLANES)
+        quant_shared(4)
+        window_with_share(5)
+        store(1, (2,), 0, CH, VECTOR)
+        quant_shared(5)
+        for m in range(MIX_TILES):
+            mix_and_store(2, (m,), 0, CH)
+
+        amplify_gpsimd(6)
+        amplify(6, 0, TAIL_SPLIT)
+        amplify(7, 0, TAIL_SPLIT)
+        quant_wave(6, 0, TAIL_SPLIT)
+        quant_wave(7, 0, TAIL_SPLIT)
+        quant_wave(6, AMP_SPLIT, CH)
+        mix_and_store(3, (0, 1), 0, TAIL_SPLIT)
+        mix_and_store(3, (2, 3), 0, TAIL_SPLIT)
+        mix_open(3, (0, 1, 2, 3), AMP_SPLIT, CH)
+        amplify(7, AMP_SPLIT, CH)
+        amplify(6, TAIL_SPLIT, AMP_SPLIT)
+        quant_wave(7, AMP_SPLIT, CH)
+        mix_close(3, (0, 1, 2, 3), AMP_SPLIT, CH)
+        store(3, (0, 1, 2, 3), AMP_SPLIT, CH, SCALAR)
+        amplify(7, TAIL_SPLIT, AMP_SPLIT)
+        quant_wave(6, TAIL_SPLIT, AMP_SPLIT)
+        mix_open(3, (0, 1), TAIL_SPLIT, AMP_SPLIT)
+        mix_open(3, (2, 3), TAIL_SPLIT, AMP_SPLIT)
+        quant_wave(7, TAIL_SPLIT, AMP_SPLIT)
+        mix_close(3, (0, 1), TAIL_SPLIT, AMP_SPLIT)
+        mix_close(3, (2, 3), TAIL_SPLIT, AMP_SPLIT)
+        store(3, (0, 1), TAIL_SPLIT, AMP_SPLIT, VECTOR)
+        store(3, (2, 3), TAIL_SPLIT, AMP_SPLIT, SCALAR)

@@ -26,8 +26,10 @@ RING_BANKS = 7
 LEAD = 4
 SINE_BUFS = 4
 GP_COLS = 320
+TURNED_BUFS = 6
+GP_AMP_FROM = {4: 336, 5: 336, 6: 384}
 AMP_SPLIT = 384
-GP_AMP_HALVES = (4, 5, 6)
+MAIN = 256
 TAIL_SPLIT = 256
 VECTOR, SCALAR = "vector", "scalar"
 
@@ -138,7 +140,9 @@ def tile_additive_sine_synthesis_s7_kernel(
             )
 
         def turn(operand, rows, i):
-            turned[operand, i] = work.tile([PART, 2, PART, 4], BF16, name="turned", tag="turned", align_bytes=64)
+            turned[operand, i] = work.tile(
+                [PART, 2, PART, 4], BF16, name="turned", tag="turned", align_bytes=64, bufs=TURNED_BUFS
+            )
             words = rows[i][:].bitcast(F32)
             bank = take_bank((operand, i), [PART, 2, 2, PART])
             for g in range(2):
@@ -195,32 +199,31 @@ def tile_additive_sine_synthesis_s7_kernel(
         def relay_tile(h, width):
             return work.tile([PART, width, 4], BF16, name="relay", tag="relay%d" % h, align_bytes=64, bufs=1)
 
+        def by_four(ap):
+            return ap.rearrange("p t (c i) -> p c t i", i=4)
+
+        def product(engine, amp_src, h, dst, n0, n1):
+            factor = amp_src[:, h % 2, :].rearrange("p (c t i) -> p c t i", c=1, i=1)
+            engine.tensor_tensor(
+                out=by_four(dst.rearrange("p n t -> p t n")),
+                in0=by_four(sine[h][:, :, n0:n1]),
+                in1=factor.to_broadcast([PART, (n1 - n0) // 4, 4, 4]),
+                op=MULT,
+            )
+
         def amplify(h, n0, n1):
             width = n1 - n0
-            if h + 1 in GP_AMP_HALVES:
+            if h + 1 in GP_AMP_FROM:
                 wave_in[h, n0] = relay_tile(h + 1, width)
             else:
                 wave_in[h, n0] = work.tile(
                     [PART, width, 4], BF16, name="wave_in", tag="wave_in", align_bytes=64, bufs=4
                 )
-            factor = amp_ps[:, h % 2, :].rearrange("p (c t i) -> p c t i", c=1, i=1)
-            nc.vector.tensor_tensor(
-                out=wave_in[h, n0][:].rearrange("p (c i) t -> p c t i", i=4),
-                in0=sine[h][:, :, n0:n1].rearrange("p t (c i) -> p c t i", i=4),
-                in1=factor.to_broadcast([PART, width // 4, 4, 4]),
-                op=MULT,
-            )
+            product(nc.vector, amp_ps, h, wave_in[h, n0][:], n0, n1)
 
-        def amplify_gpsimd(h):
-            width = CH - AMP_SPLIT
-            wave_in[h, AMP_SPLIT] = relay_tile(h, width)
-            factor = amp_sb[:, h % 2, :].rearrange("p (n t) -> p n t", n=1)
-            nc.gpsimd.tensor_tensor(
-                out=wave_in[h, AMP_SPLIT][:],
-                in0=sine[h][:, :, AMP_SPLIT:CH].rearrange("p t n -> p n t"),
-                in1=factor.to_broadcast([PART, width, 4]),
-                op=MULT,
-            )
+        def amplify_gpsimd(h, n0):
+            wave_in[h, n0] = relay_tile(h, CH - n0)
+            product(nc.gpsimd, amp_sb, h, wave_in[h, n0][:, GP_AMP_FROM[h] - n0 :, :], GP_AMP_FROM[h], CH)
 
         def quant_wave(h, n0, n1):
             if h not in wave_codes:
@@ -282,12 +285,13 @@ def tile_additive_sine_synthesis_s7_kernel(
             interleave(h + LEAD, CH - GP_COLS)
 
         def window_with_share(h):
-            amplify_gpsimd(h)
-            amplify(h, 0, AMP_SPLIT)
+            amplify_gpsimd(h, MAIN)
+            amplify(h, 0, MAIN)
+            product(nc.vector, amp_ps, h, wave_in[h, MAIN][:, : GP_AMP_FROM[h] - MAIN, :], MAIN, GP_AMP_FROM[h])
 
         def quant_shared(h):
-            quant_wave(h, 0, AMP_SPLIT)
-            quant_wave(h, AMP_SPLIT, CH)
+            quant_wave(h, 0, MAIN)
+            quant_wave(h, MAIN, CH)
 
         load_by_plane(nc.scalar, row_scale, basis_scale.rearrange("(g p t) o -> p g (t o)", p=PART, t=4))
         nc.gpsimd.memset(table_warm[:], 0.0)
@@ -423,7 +427,7 @@ def tile_additive_sine_synthesis_s7_kernel(
         for m in range(MIX_TILES):
             mix_and_store(2, (m,), 0, CH)
 
-        amplify_gpsimd(6)
+        amplify_gpsimd(6, AMP_SPLIT)
         amplify(6, 0, TAIL_SPLIT)
         amplify(7, 0, TAIL_SPLIT)
         quant_wave(6, 0, TAIL_SPLIT)

@@ -25,12 +25,11 @@ MIX_TILES = C // PART
 RING_BANKS = 7
 LEAD = 4
 SINE_BUFS = 4
-GP_COLS = 320
+GP_COLS = 384
 TURNED_BUFS = 6
-GP_AMP_FROM = {4: 336, 5: 336, 6: 384}
-AMP_SPLIT = 384
+GP_AMP_FROM = {4: 336, 5: 336, 6: 288}
+LAST = 384
 MAIN = 256
-TAIL_SPLIT = 256
 VECTOR, SCALAR = "vector", "scalar"
 
 
@@ -85,6 +84,9 @@ def tile_additive_sine_synthesis_s7_kernel(
         def give_bank(key):
             free_banks.append(bank_of[key])
 
+        def by_four(ap):
+            return ap.rearrange("p t (c i) -> p c t i", i=4)
+
         def load_basis(b, planes=slice(0, 4)):
             c, g = b // 2, b % 2
             held = PLANES[planes]
@@ -124,8 +126,8 @@ def tile_additive_sine_synthesis_s7_kernel(
         def interleave_gpsimd(b, n0):
             basis_in[b] = work.tile([PART, CH, 4], BF16, name="basis_gp", tag="basis_gp", align_bytes=64, bufs=1)
             nc.gpsimd.tensor_scalar(
-                out=basis_in[b][:, n0:CH, :],
-                in0=wide[b][:, :, n0:CH].rearrange("p t n -> p n t"),
+                out=by_four(basis_in[b][:, n0:CH, :].rearrange("p n t -> p t n")),
+                in0=by_four(wide[b][:, :, n0:CH]),
                 scalar1=1.0,
                 scalar2=0.0,
                 op0=MULT,
@@ -174,33 +176,30 @@ def tile_additive_sine_synthesis_s7_kernel(
         def quant_mix(m):
             quant_turned("mix", mix_codes, mix_scales, m)
 
-        def sines(h, planes):
+        def sines(h, planes, n0=0, n1=CH):
             c, half = h // 2, h % 2
             if h not in sine:
                 sine[h] = work.tile([PART, 4, CH], F32, name="sine", tag="sine", bufs=SINE_BUFS)
             for t in planes:
-                bank = take_bank(("phase", h, t), [PART, CH])
+                bank = take_bank(("phase", h, t), [PART, n1 - n0])
                 i = 4 * half + t
                 for g in range(2):
                     nc.tensor.matmul_mx(
                         out=bank[:],
                         lhsT=freq_codes[:, i, PART * g : PART * (g + 1)].bitcast(FP8X4),
                         lhsT_scale=freq_scales[:, i, PART * g : PART * (g + 1)],
-                        rhs=basis_codes[:, 2 * c + g, :].bitcast(FP8X4),
-                        rhs_scale=basis_scales[:, 2 * c + g, :],
+                        rhs=basis_codes[:, 2 * c + g, n0:n1].bitcast(FP8X4),
+                        rhs_scale=basis_scales[:, 2 * c + g, n0:n1],
                         start=(g == 0),
                         stop=(g == 1),
                     )
                 nc.scalar.activation(
-                    out=sine[h][:, t, :], in_=bank[:], func=ACTF.Sin, bias=onset_sb[:, half, t : t + 1]
+                    out=sine[h][:, t, n0:n1], in_=bank[:], func=ACTF.Sin, bias=onset_sb[:, half, t : t + 1]
                 )
                 give_bank(("phase", h, t))
 
         def relay_tile(h, width):
             return work.tile([PART, width, 4], BF16, name="relay", tag="relay%d" % h, align_bytes=64, bufs=1)
-
-        def by_four(ap):
-            return ap.rearrange("p t (c i) -> p c t i", i=4)
 
         def product(engine, amp_src, h, dst, n0, n1):
             factor = amp_src[:, h % 2, :].rearrange("p (c t i) -> p c t i", c=1, i=1)
@@ -221,9 +220,12 @@ def tile_additive_sine_synthesis_s7_kernel(
                 )
             product(nc.vector, amp_ps, h, wave_in[h, n0][:], n0, n1)
 
-        def amplify_gpsimd(h, n0):
-            wave_in[h, n0] = relay_tile(h, CH - n0)
-            product(nc.gpsimd, amp_sb, h, wave_in[h, n0][:, GP_AMP_FROM[h] - n0 :, :], GP_AMP_FROM[h], CH)
+        def amplify_gpsimd(h, n0, n1=CH):
+            wave_in[h, n0] = relay_tile(h, n1 - n0)
+            product(nc.gpsimd, amp_sb, h, wave_in[h, n0][:, GP_AMP_FROM[h] - n0 :, :], GP_AMP_FROM[h], n1)
+
+        def amplify_rest(h):
+            product(nc.vector, amp_ps, h, wave_in[h, MAIN][:, : GP_AMP_FROM[h] - MAIN, :], MAIN, GP_AMP_FROM[h])
 
         def quant_wave(h, n0, n1):
             if h not in wave_codes:
@@ -287,7 +289,7 @@ def tile_additive_sine_synthesis_s7_kernel(
         def window_with_share(h):
             amplify_gpsimd(h, MAIN)
             amplify(h, 0, MAIN)
-            product(nc.vector, amp_ps, h, wave_in[h, MAIN][:, : GP_AMP_FROM[h] - MAIN, :], MAIN, GP_AMP_FROM[h])
+            amplify_rest(h)
 
         def quant_shared(h):
             quant_wave(h, 0, MAIN)
@@ -365,9 +367,9 @@ def tile_additive_sine_synthesis_s7_kernel(
         quant_basis(3)
 
         sines(1, PLANES)
-        widen(5, (2, 3), SCALAR)
+        widen(5, (3,), SCALAR)
         window_with_basis(0)
-        widen(5, (0, 1), VECTOR)
+        widen(5, (0, 1, 2), VECTOR)
         quant_basis(4)
         quant_wave(0, 0, CH)
 
@@ -423,30 +425,26 @@ def tile_additive_sine_synthesis_s7_kernel(
         quant_shared(4)
         window_with_share(5)
         store(1, (2,), 0, CH, VECTOR)
+
         quant_shared(5)
+
         for m in range(MIX_TILES):
             mix_and_store(2, (m,), 0, CH)
-
-        amplify_gpsimd(6, AMP_SPLIT)
-        amplify(6, 0, TAIL_SPLIT)
-        amplify(7, 0, TAIL_SPLIT)
-        quant_wave(6, 0, TAIL_SPLIT)
-        quant_wave(7, 0, TAIL_SPLIT)
-        quant_wave(6, AMP_SPLIT, CH)
-        mix_and_store(3, (0, 1), 0, TAIL_SPLIT)
-        mix_and_store(3, (2, 3), 0, TAIL_SPLIT)
-        mix_open(3, (0, 1, 2, 3), AMP_SPLIT, CH)
-        amplify(7, AMP_SPLIT, CH)
-        amplify(6, TAIL_SPLIT, AMP_SPLIT)
-        quant_wave(7, AMP_SPLIT, CH)
-        mix_close(3, (0, 1, 2, 3), AMP_SPLIT, CH)
-        store(3, (0, 1, 2, 3), AMP_SPLIT, CH, SCALAR)
-        amplify(7, TAIL_SPLIT, AMP_SPLIT)
-        quant_wave(6, TAIL_SPLIT, AMP_SPLIT)
-        mix_open(3, (0, 1), TAIL_SPLIT, AMP_SPLIT)
-        mix_open(3, (2, 3), TAIL_SPLIT, AMP_SPLIT)
-        quant_wave(7, TAIL_SPLIT, AMP_SPLIT)
-        mix_close(3, (0, 1), TAIL_SPLIT, AMP_SPLIT)
-        mix_close(3, (2, 3), TAIL_SPLIT, AMP_SPLIT)
-        store(3, (0, 1), TAIL_SPLIT, AMP_SPLIT, VECTOR)
-        store(3, (2, 3), TAIL_SPLIT, AMP_SPLIT, SCALAR)
+        amplify_gpsimd(6, MAIN)
+        amplify(6, 0, MAIN)
+        amplify_rest(6)
+        amplify(7, 0, MAIN)
+        quant_wave(6, 0, MAIN)
+        quant_wave(7, 0, MAIN)
+        mix_and_store(3, (0, 1), 0, MAIN)
+        mix_and_store(3, (2, 3), 0, MAIN)
+        quant_wave(6, MAIN, CH)
+        for m in range(MIX_TILES):
+            mix_open(3, (m,), MAIN, CH)
+        amplify(7, MAIN, LAST)
+        amplify(7, LAST, CH)
+        quant_wave(7, MAIN, LAST)
+        quant_wave(7, LAST, CH)
+        for m in range(MIX_TILES):
+            mix_close(3, (m,), MAIN, CH)
+            store(3, (m,), MAIN, CH, VECTOR if m % 2 == 0 else SCALAR)

@@ -25,7 +25,7 @@ MIX_TILES = C // PART
 RING_BANKS = 7
 LEAD = 4
 SINE_BUFS = 4
-GP_COLS = 384
+GP_FROM = 128
 TURNED_BUFS = 6
 GP_AMP_FROM = {4: 336, 5: 336, 6: 288}
 LAST = 384
@@ -77,9 +77,9 @@ def tile_additive_sine_synthesis_s7_kernel(
         free_banks = list(range(RING_BANKS))
         bank_of = {}
 
-        def take_bank(key, shape):
+        def take_bank(key, shape, dtype=F32):
             bank_of[key] = free_banks.pop(0)
-            return psum.tile(shape, F32, name="bank", tag="bank%d" % bank_of[key])
+            return psum.tile(shape, dtype, name="bank", tag="bank%d" % bank_of[key])
 
         def give_bank(key):
             free_banks.append(bank_of[key])
@@ -115,30 +115,44 @@ def tile_additive_sine_synthesis_s7_kernel(
                 else:
                     nc.scalar.activation(out=wide[b][:, t, :], in_=src, func=ACTF.Copy, scale=factor)
 
-        def interleave(b, n1):
-            if b < LEAD:
-                basis_in[b] = work.tile([PART, CH, 4], BF16, name="basis_in", tag="basis_in", align_bytes=64, bufs=2)
-            nc.vector.tensor_copy(
-                out=basis_in[b][:, 0:n1, :].rearrange("p (c i) t -> p c t i", i=4),
-                in_=wide[b][:, :, 0:n1].rearrange("p t (c i) -> p c t i", i=4),
-            )
+        def interleave(b):
+            basis_in[b, 0] = work.tile([PART, CH, 4], BF16, name="basis_in", tag="basis_in", align_bytes=64, bufs=2)
+            nc.vector.tensor_copy(out=by_four(basis_in[b, 0][:].rearrange("p n t -> p t n")), in_=by_four(wide[b][:]))
 
-        def interleave_gpsimd(b, n0):
-            basis_in[b] = work.tile([PART, CH, 4], BF16, name="basis_gp", tag="basis_gp", align_bytes=64, bufs=1)
+        def interleave_tensor(b):
+            basis_in[b, 0] = work.tile([PART, GP_FROM, 4], BF16, name="basis_pe", tag="basis_pe", align_bytes=64)
+            bank = take_bank(("basis", b), [PART, GP_FROM, 4], BF16)
+            nc.tensor.matmul(
+                bank[:],
+                lhsT=ident_bf[:],
+                rhs=wide[b][:, :, 0:GP_FROM].rearrange("p t n -> p n t"),
+                start=True,
+                stop=True,
+            )
+            nc.scalar.copy(
+                out=basis_in[b, 0][:].rearrange("p n t -> p (n t)").bitcast(F32),
+                in_=bank[:].rearrange("p n t -> p (n t)").bitcast(F32),
+            )
+            give_bank(("basis", b))
+
+        def interleave_gpsimd(b):
+            basis_in[b, GP_FROM] = work.tile(
+                [PART, CH - GP_FROM, 4], BF16, name="basis_gp", tag="basis_gp", align_bytes=64, bufs=1
+            )
             nc.gpsimd.tensor_scalar(
-                out=by_four(basis_in[b][:, n0:CH, :].rearrange("p n t -> p t n")),
-                in0=by_four(wide[b][:, :, n0:CH]),
+                out=by_four(basis_in[b, GP_FROM][:].rearrange("p n t -> p t n")),
+                in0=by_four(wide[b][:, :, GP_FROM:CH]),
                 scalar1=1.0,
                 scalar2=0.0,
                 op0=MULT,
                 op1=ADD,
             )
 
-        def quant_basis(b):
+        def quant_basis(b, n0=0, n1=CH):
             nc.vector.quantize_mx(
-                out=basis_codes[:, b, :].bitcast(FP8X4),
-                scales=basis_scales[:, b, :],
-                in_=basis_in[b][:].rearrange("p n t -> p (n t)"),
+                out=basis_codes[:, b, n0:n1].bitcast(FP8X4),
+                scales=basis_scales[:, b, n0:n1],
+                in_=basis_in[b, n0][:].rearrange("p n t -> p (n t)"),
             )
 
         def turn(operand, rows, i):
@@ -282,9 +296,8 @@ def tile_additive_sine_synthesis_s7_kernel(
             store(c, tiles, n0, n1, SCALAR)
 
         def window_with_basis(h):
-            interleave_gpsimd(h + LEAD, CH - GP_COLS)
+            interleave_gpsimd(h + LEAD)
             amplify(h, 0, CH)
-            interleave(h + LEAD, CH - GP_COLS)
 
         def window_with_share(h):
             amplify_gpsimd(h, MAIN)
@@ -331,15 +344,15 @@ def tile_additive_sine_synthesis_s7_kernel(
         widen(2, (3,), SCALAR)
         for i in range(1, 4):
             turn_freq(i)
-        interleave(0, CH)
-        interleave(1, CH)
+        interleave(0)
+        interleave(1)
         quant_basis(0)
         quant_freq(0)
         quant_basis(1)
         quant_freq(1)
         widen(3, (0, 1), VECTOR)
         quant_freq(2)
-        interleave(2, CH)
+        interleave(2)
         quant_freq(3)
         widen(3, (2,), SCALAR)
         sines(0, (0,))
@@ -356,7 +369,7 @@ def tile_additive_sine_synthesis_s7_kernel(
             stop=True,
         )
         quant_basis(2)
-        interleave(3, CH)
+        interleave(3)
         widen(4, (0, 1), VECTOR)
         quant_freq(4)
         quant_freq(5)
@@ -367,50 +380,58 @@ def tile_additive_sine_synthesis_s7_kernel(
         quant_basis(3)
 
         sines(1, PLANES)
+        interleave_tensor(4)
         widen(5, (3,), SCALAR)
         window_with_basis(0)
         widen(5, (0, 1, 2), VECTOR)
-        quant_basis(4)
+        quant_basis(4, 0, GP_FROM)
+        quant_basis(4, GP_FROM, CH)
         quant_wave(0, 0, CH)
 
         sines(2, (0, 1))
         turn_mix(0)
         turn_mix(1)
         sines(2, (2, 3))
-        widen(6, (2, 3), SCALAR)
+        interleave_tensor(5)
+        widen(6, (3,), SCALAR)
         window_with_basis(1)
-        widen(6, (0, 1), VECTOR)
+        widen(6, (0, 1, 2), VECTOR)
         quant_mix(0)
         quant_mix(1)
-        quant_basis(5)
+        quant_basis(5, 0, GP_FROM)
+        quant_basis(5, GP_FROM, CH)
         quant_wave(1, 0, CH)
 
         sines(3, PLANES)
         turn_mix(2)
         turn_mix(3)
-        widen(7, (2, 3), SCALAR)
+        interleave_tensor(6)
+        widen(7, (3,), SCALAR)
         sines(4, (0, 1))
         mix_bank(0, (0,), 0, CH)
         mix_bank(0, (1,), 0, CH)
         sines(4, (2, 3))
         window_with_basis(2)
-        widen(7, (0, 1), VECTOR)
+        widen(7, (0, 1, 2), VECTOR)
         quant_mix(2)
         quant_mix(3)
-        quant_basis(6)
+        quant_basis(6, 0, GP_FROM)
+        quant_basis(6, GP_FROM, CH)
         quant_wave(2, 0, CH)
 
         store(0, (0,), 0, CH, SCALAR)
         store(0, (1,), 0, CH, SCALAR)
         sines(5, (0, 1))
+        interleave_tensor(7)
         mix_and_store(0, (2,), 0, CH)
         sines(5, (2, 3))
         mix_and_store(0, (3,), 0, CH)
         for m in range(MIX_TILES):
             mix_open(1, (m,), 0, CH)
         window_with_basis(3)
+        quant_basis(7, 0, GP_FROM)
         quant_wave(3, 0, CH)
-        quant_basis(7)
+        quant_basis(7, GP_FROM, CH)
 
         mix_close(1, (0,), 0, CH)
         store(1, (0,), 0, CH, SCALAR)

@@ -46,6 +46,7 @@ def tile_additive_sine_synthesis_s7_kernel(
         ident = keep.tile([PART, PART], F32, name="ident")
         ident_bf = keep.tile([PART, PART], BF16, name="ident_bf")
         table_warm = keep.tile([PART, 1], F32, name="table_warm")
+        ramp = keep.tile([PART, CH], BF16, name="ramp")
         row_scale = keep.tile([PART, 2, 4], F32, name="row_scale")
         onset_sb = keep.tile([PART, 2, 4], BF16, name="onset_sb")
         amp_sb = keep.tile([PART, 2, 4], BF16, name="amp_sb")
@@ -154,6 +155,12 @@ def tile_additive_sine_synthesis_s7_kernel(
                 scales=basis_scales[:, b, n0:n1],
                 in_=basis_in[b, n0][:].rearrange("p n t -> p (n t)"),
             )
+
+        def warm_tensor(*sources):
+            bank = take_bank("warm", [PART, CH])
+            for src in sources:
+                nc.tensor.matmul(bank[:], lhsT=ident_bf[:], rhs=src, start=True, stop=True)
+            give_bank("warm")
 
         def turn(operand, rows, i):
             turned[operand, i] = work.tile(
@@ -310,6 +317,7 @@ def tile_additive_sine_synthesis_s7_kernel(
 
         load_by_plane(nc.scalar, row_scale, basis_scale.rearrange("(g p t) o -> p g (t o)", p=PART, t=4))
         nc.gpsimd.memset(table_warm[:], 0.0)
+        nc.gpsimd.memset(ramp[:], 0.0)
         make_identity(nc, ident[:])
         make_identity(nc, ident_bf[:])
         nc.scalar.activation(out=table_warm[:], in_=table_warm[:], func=ACTF.Sin)
@@ -340,10 +348,13 @@ def tile_additive_sine_synthesis_s7_kernel(
         widen(1, (0, 1, 2), VECTOR)
         widen(1, (3,), SCALAR)
         widen(2, (0, 1, 2), SCALAR)
+        warm_tensor(ramp[:], ramp[:], ramp[:], wide[0][:, 0, :], wide[0][:, 2, :], wide[0][:, 1, :], wide[0][:, 3, :])
         turn_freq(0)
         widen(2, (3,), SCALAR)
-        for i in range(1, 4):
-            turn_freq(i)
+        turn_freq(1)
+        warm_tensor(ramp[:], ramp[:])
+        turn_freq(2)
+        turn_freq(3)
         interleave(0)
         interleave(1)
         quant_basis(0)
@@ -357,9 +368,12 @@ def tile_additive_sine_synthesis_s7_kernel(
         widen(3, (2,), SCALAR)
         sines(0, (0,))
         widen(3, (3,), SCALAR)
-        sines(0, (1, 2))
-        for i in range(4, FREQ_TILES):
-            turn_freq(i)
+        sines(0, (1,))
+        turn_freq(4)
+        turn_freq(5)
+        sines(0, (2,))
+        turn_freq(6)
+        turn_freq(7)
         sines(0, (3,))
         nc.tensor.matmul(
             amp_ps[:].rearrange("p g t -> p (g t)"),
@@ -402,9 +416,10 @@ def tile_additive_sine_synthesis_s7_kernel(
         quant_basis(5, GP_FROM, CH)
         quant_wave(1, 0, CH)
 
-        sines(3, PLANES)
+        sines(3, (0, 1))
         turn_mix(2)
         turn_mix(3)
+        sines(3, (2, 3))
         interleave_tensor(6)
         widen(7, (3,), SCALAR)
         sines(4, (0, 1))

@@ -22,11 +22,11 @@ CH = 512
 HALVES = 2 * T // CH
 FREQ_TILES = P // PART
 MIX_TILES = C // PART
-RING_BANKS = 7
+RING_BANKS = 8
 LEAD = 4
 SINE_BUFS = 4
 GP_FROM = 128
-TURNED_BUFS = 6
+TURNED_BUFS = 3
 GP_AMP_FROM = {4: 336, 5: 336, 6: 288}
 LAST = 384
 MAIN = 256
@@ -46,11 +46,9 @@ def tile_additive_sine_synthesis_s7_kernel(
         ident = keep.tile([PART, PART], F32, name="ident")
         ident_bf = keep.tile([PART, PART], BF16, name="ident_bf")
         table_warm = keep.tile([PART, 1], F32, name="table_warm")
-        ramp = keep.tile([PART, CH], BF16, name="ramp")
         row_scale = keep.tile([PART, 2, 4], F32, name="row_scale")
         onset_sb = keep.tile([PART, 2, 4], BF16, name="onset_sb")
         amp_sb = keep.tile([PART, 2, 4], BF16, name="amp_sb")
-        amp_ps = psum.tile([PART, 2, 4], F32, name="amp_ps", tag="amp_ps")
         freq_rows = [keep.tile([PART, K], BF16, name="freq_rows%d" % i, align_bytes=64) for i in range(FREQ_TILES)]
         mix_rows = [keep.tile([PART, P], BF16, name="mix_rows%d" % m, align_bytes=64) for m in range(MIX_TILES)]
         freq_codes = keep.tile([PART, FREQ_TILES, 2 * PART], U32, name="freq_codes", align_bytes=64)
@@ -65,9 +63,13 @@ def tile_additive_sine_synthesis_s7_kernel(
         mix_v = mix.rearrange("(i m) k -> i m k", m=PART)
         out_v = out.rearrange("(m p) n -> p m n", p=PART)
 
+        factors = {}
+        pieces = {}
         raw = {}
         wide = {}
         basis_in = {}
+        turn_bank = {}
+        basis_bank = {}
         turned = {}
         sine = {}
         wave_in = {}
@@ -93,6 +95,7 @@ def tile_additive_sine_synthesis_s7_kernel(
             held = PLANES[planes]
             piece = keep.tile([PART, len(held), CH], U8, name="raw%d_%d" % (b, held[0]))
             nc.sync.dma_start(out=piece[:], in_=basis_v[g, :, planes, c * CH : (c + 1) * CH])
+            pieces[b, held[0]] = piece
             for j, t in enumerate(held):
                 raw[b, t] = piece[:, j, :]
 
@@ -107,7 +110,7 @@ def tile_additive_sine_synthesis_s7_kernel(
 
         def widen(b, planes, engine):
             if b not in wide:
-                wide[b] = work.tile([PART, 4, CH], BF16, name="wide", tag="wide", align_bytes=64)
+                wide[b] = work.tile([PART, 4, CH], BF16, name="wide", tag="wide", align_bytes=64, bufs=4)
             for t in planes:
                 src = raw[b, t].bitcast(FP8)
                 factor = row_scale[:, b % 2, t : t + 1]
@@ -116,9 +119,69 @@ def tile_additive_sine_synthesis_s7_kernel(
                 else:
                     nc.scalar.activation(out=wide[b][:, t, :], in_=src, func=ACTF.Copy, scale=factor)
 
-        def interleave(b):
-            basis_in[b, 0] = work.tile([PART, CH, 4], BF16, name="basis_in", tag="basis_in", align_bytes=64, bufs=2)
-            nc.vector.tensor_copy(out=by_four(basis_in[b, 0][:].rearrange("p n t -> p t n")), in_=by_four(wide[b][:]))
+        def cast(b, first, count):
+            if b not in wide:
+                wide[b] = work.tile([PART, 4, CH], BF16, name="wide", tag="wide", align_bytes=64, bufs=4)
+            nc.scalar.copy(
+                out=wide[b][:, first : first + count, :].rearrange("p t n -> p (t n)"),
+                in_=pieces[b, first][:].rearrange("p t n -> p (t n)").bitcast(FP8),
+            )
+
+        def factor_to_psum(key, identity, src):
+            factors[key] = take_bank(key, [PART, 2, 4])
+            nc.tensor.matmul(
+                factors[key][:].rearrange("p g t -> p (g t)"),
+                lhsT=identity[:],
+                rhs=src[:].rearrange("p g t -> p (g t)"),
+                start=True,
+                stop=True,
+            )
+
+        def scale_and_interleave(b):
+            whole_tile(b)
+            factor = factors["scale"][:, b % 2, :].rearrange("p (c t i) -> p c t i", c=1, i=1)
+            nc.vector.tensor_tensor(
+                out=by_four(basis_in[b, 0][:].rearrange("p n t -> p t n")),
+                in0=by_four(wide[b][:]),
+                in1=factor.to_broadcast([PART, CH // 4, 4, 4]),
+                op=MULT,
+            )
+
+        def whole_tile(b):
+            if (b, 0) not in basis_in:
+                basis_in[b, 0] = work.tile(
+                    [PART, CH, 4], BF16, name="basis_in", tag="basis_in", align_bytes=64, bufs=3
+                )
+            return basis_in[b, 0]
+
+        def interleave(b, n1=CH):
+            nc.vector.tensor_copy(
+                out=by_four(whole_tile(b)[:, :n1, :].rearrange("p n t -> p t n")), in_=by_four(wide[b][:, :, :n1])
+            )
+
+        def fill_bank(b, n0, n1):
+            basis_bank[b] = take_bank(("basis", b), [PART, n1 - n0, 4], BF16)
+            for n in range(n0, n1, PART):
+                nc.tensor.matmul(
+                    basis_bank[b][:, n - n0 : n - n0 + PART, :],
+                    lhsT=ident_bf[:],
+                    rhs=wide[b][:, :, n : n + PART].rearrange("p t n -> p n t"),
+                    start=True,
+                    stop=True,
+                )
+
+        def empty_bank(b, n0, n1):
+            nc.scalar.copy(
+                out=whole_tile(b)[:, n0:n1, :].rearrange("p n t -> p (n t)").bitcast(F32),
+                in_=basis_bank[b][:].rearrange("p n t -> p (n t)").bitcast(F32),
+            )
+            give_bank(("basis", b))
+
+        def interleave_rest(b):
+            basis_in[b, 0] = work.tile([PART, GP_FROM, 4], BF16, name="basis_pe", tag="basis_pe", align_bytes=64)
+            nc.vector.tensor_copy(
+                out=by_four(basis_in[b, 0][:].rearrange("p n t -> p t n")), in_=by_four(wide[b][:, :, :GP_FROM])
+            )
 
         def interleave_tensor(b):
             basis_in[b, 0] = work.tile([PART, GP_FROM, 4], BF16, name="basis_pe", tag="basis_pe", align_bytes=64)
@@ -136,13 +199,13 @@ def tile_additive_sine_synthesis_s7_kernel(
             )
             give_bank(("basis", b))
 
-        def interleave_gpsimd(b):
-            basis_in[b, GP_FROM] = work.tile(
-                [PART, CH - GP_FROM, 4], BF16, name="basis_gp", tag="basis_gp", align_bytes=64, bufs=1
+        def interleave_gpsimd(b, n0=GP_FROM):
+            basis_in[b, n0] = work.tile(
+                [PART, CH - n0, 4], BF16, name="basis_gp", tag="basis_gp", align_bytes=64, bufs=1
             )
             nc.gpsimd.tensor_scalar(
-                out=by_four(basis_in[b, GP_FROM][:].rearrange("p n t -> p t n")),
-                in0=by_four(wide[b][:, :, GP_FROM:CH]),
+                out=by_four(basis_in[b, n0][:].rearrange("p n t -> p t n")),
+                in0=by_four(wide[b][:, :, n0:CH]),
                 scalar1=1.0,
                 scalar2=0.0,
                 op0=MULT,
@@ -156,46 +219,51 @@ def tile_additive_sine_synthesis_s7_kernel(
                 in_=basis_in[b, n0][:].rearrange("p n t -> p (n t)"),
             )
 
-        def warm_tensor(*sources):
+        def warm_tensor(identity, *sources):
             bank = take_bank("warm", [PART, CH])
             for src in sources:
-                nc.tensor.matmul(bank[:], lhsT=ident_bf[:], rhs=src, start=True, stop=True)
+                nc.tensor.matmul(bank[:, : src.shape[1]], lhsT=identity[:], rhs=src, start=True, stop=True)
             give_bank("warm")
 
-        def turn(operand, rows, i):
-            turned[operand, i] = work.tile(
-                [PART, 2, PART, 4], BF16, name="turned", tag="turned", align_bytes=64, bufs=TURNED_BUFS
-            )
+        def turn(operand, rows, i, engine):
+            if i % 2 == 0:
+                turned[operand, i // 2] = work.tile(
+                    [PART, 2, 2, PART, 4], BF16, name="turned", tag="turned", align_bytes=64, bufs=TURNED_BUFS
+                )
             words = rows[i][:].bitcast(F32)
             bank = take_bank((operand, i), [PART, 2, 2, PART])
             for g in range(2):
                 for u in range(2):
                     nc.tensor.transpose(bank[:, g, u, :], words[:, 256 * g + u : 256 * (g + 1) : 2], ident[:])
-            dst = turned[operand, i][:].rearrange("p g r t -> p (g r t)").bitcast(F32)
-            nc.scalar.copy(
-                out=dst.rearrange("p (g r u) -> p g r u", g=2, u=2),
-                in_=bank[:].rearrange("p g u r -> p g r u"),
-            )
+            turn_bank[operand, i] = bank
+            if engine is not None:
+                empty_turned(operand, i, engine)
+
+        def empty_turned(operand, i, engine):
+            bank = turn_bank[operand, i]
+            dst = turned[operand, i // 2][:, i % 2].rearrange("p g r t -> p (g r t)").bitcast(F32)
+            copy = nc.vector.tensor_copy if engine == VECTOR else nc.scalar.copy
+            copy(out=dst.rearrange("p (g r u) -> p g r u", g=2, u=2), in_=bank[:].rearrange("p g u r -> p g r u"))
             give_bank((operand, i))
 
-        def quant_turned(operand, codes, scales, i):
+        def quant_turned(operand, codes, scales, i, count):
             nc.vector.quantize_mx(
-                out=codes[:, i, :].bitcast(FP8X4),
-                scales=scales[:, i, :],
-                in_=turned[operand, i][:].rearrange("p g r t -> p (g r t)"),
+                out=codes[:, i : i + count, :].rearrange("p i r -> p (i r)").bitcast(FP8X4),
+                scales=scales[:, i : i + count, :].rearrange("p i r -> p (i r)"),
+                in_=turned[operand, i // 2][:, i % 2 : i % 2 + count].rearrange("p i g r t -> p (i g r t)"),
             )
 
-        def turn_freq(i):
-            turn("freq", freq_rows, i)
+        def turn_freq(i, engine=SCALAR):
+            turn("freq", freq_rows, i, engine)
 
-        def turn_mix(m):
-            turn("mix", mix_rows, m)
+        def turn_mix(m, engine=SCALAR):
+            turn("mix", mix_rows, m, engine)
 
-        def quant_freq(i):
-            quant_turned("freq", freq_codes, freq_scales, i)
+        def quant_freq(i, count=1):
+            quant_turned("freq", freq_codes, freq_scales, i, count)
 
-        def quant_mix(m):
-            quant_turned("mix", mix_codes, mix_scales, m)
+        def quant_mix(m, count=1):
+            quant_turned("mix", mix_codes, mix_scales, m, count)
 
         def sines(h, planes, n0=0, n1=CH):
             c, half = h // 2, h % 2
@@ -239,14 +307,14 @@ def tile_additive_sine_synthesis_s7_kernel(
                 wave_in[h, n0] = work.tile(
                     [PART, width, 4], BF16, name="wave_in", tag="wave_in", align_bytes=64, bufs=4
                 )
-            product(nc.vector, amp_ps, h, wave_in[h, n0][:], n0, n1)
+            product(nc.vector, factors["amp"], h, wave_in[h, n0][:], n0, n1)
 
         def amplify_gpsimd(h, n0, n1=CH):
             wave_in[h, n0] = relay_tile(h, n1 - n0)
             product(nc.gpsimd, amp_sb, h, wave_in[h, n0][:, GP_AMP_FROM[h] - n0 :, :], GP_AMP_FROM[h], n1)
 
         def amplify_rest(h):
-            product(nc.vector, amp_ps, h, wave_in[h, MAIN][:, : GP_AMP_FROM[h] - MAIN, :], MAIN, GP_AMP_FROM[h])
+            product(nc.vector, factors["amp"], h, wave_in[h, MAIN][:, : GP_AMP_FROM[h] - MAIN, :], MAIN, GP_AMP_FROM[h])
 
         def quant_wave(h, n0, n1):
             if h not in wave_codes:
@@ -317,22 +385,19 @@ def tile_additive_sine_synthesis_s7_kernel(
 
         load_by_plane(nc.scalar, row_scale, basis_scale.rearrange("(g p t) o -> p g (t o)", p=PART, t=4))
         nc.gpsimd.memset(table_warm[:], 0.0)
-        nc.gpsimd.memset(ramp[:], 0.0)
         make_identity(nc, ident[:])
         make_identity(nc, ident_bf[:])
         nc.scalar.activation(out=table_warm[:], in_=table_warm[:], func=ACTF.Sin)
-
         load_basis(0, slice(0, 1))
         load_basis(0, slice(2, 3))
         load_basis(0, slice(1, 4, 2))
         load_basis(1, slice(0, 2))
         load_basis(1, slice(2, 4))
         load_basis(2)
-        for i in range(3):
+        for i in range(4):
             load_freq(i)
-        load_by_plane(nc.sync, onset_sb, onset.rearrange("(g p t) -> p g t", p=PART, t=4))
-        load_freq(3)
         load_basis(3)
+        load_by_plane(nc.sync, onset_sb, onset.rearrange("(g p t) -> p g t", p=PART, t=4))
         for i in range(4, FREQ_TILES):
             load_freq(i)
         load_basis(4)
@@ -347,51 +412,49 @@ def tile_additive_sine_synthesis_s7_kernel(
         widen(0, (2, 3), SCALAR)
         widen(1, (0, 1, 2), VECTOR)
         widen(1, (3,), SCALAR)
-        widen(2, (0, 1, 2), SCALAR)
-        warm_tensor(ramp[:], ramp[:], ramp[:], wide[0][:, 0, :], wide[0][:, 2, :], wide[0][:, 1, :], wide[0][:, 3, :])
+        cast(2, 0, 4)
+        warm_tensor(ident, ident[:], ident[:], ident[:])
+        factor_to_psum("scale", ident, row_scale)
+        warm_tensor(ident_bf, wide[0][:, 0, :], wide[0][:, 2, :], wide[0][:, 1, :], wide[0][:, 3, :])
+        interleave(0)
+        interleave(1, MAIN)
+        fill_bank(1, MAIN, CH)
+        empty_bank(1, MAIN, CH)
         turn_freq(0)
-        widen(2, (3,), SCALAR)
         turn_freq(1)
-        warm_tensor(ramp[:], ramp[:])
         turn_freq(2)
         turn_freq(3)
-        interleave(0)
-        interleave(1)
+        widen(3, (0,), SCALAR)
+
         quant_basis(0)
-        quant_freq(0)
         quant_basis(1)
+        quant_freq(0)
         quant_freq(1)
-        widen(3, (0, 1), VECTOR)
+        widen(3, (1, 2), VECTOR)
         quant_freq(2)
-        interleave(2)
+        widen(3, (3,), VECTOR)
         quant_freq(3)
-        widen(3, (2,), SCALAR)
-        sines(0, (0,))
-        widen(3, (3,), SCALAR)
-        sines(0, (1,))
+        interleave_gpsimd(3)
+        scale_and_interleave(2)
+        give_bank("scale")
+        sines(0, (0, 1))
         turn_freq(4)
         turn_freq(5)
         sines(0, (2,))
         turn_freq(6)
         turn_freq(7)
+        interleave_tensor(3)
+        widen(4, (0,), SCALAR)
         sines(0, (3,))
-        nc.tensor.matmul(
-            amp_ps[:].rearrange("p g t -> p (g t)"),
-            lhsT=ident_bf[:],
-            rhs=amp_sb[:].rearrange("p g t -> p (g t)"),
-            start=True,
-            stop=True,
-        )
-        quant_basis(2)
-        interleave(3)
-        widen(4, (0, 1), VECTOR)
-        quant_freq(4)
-        quant_freq(5)
+        factor_to_psum("amp", ident_bf, amp_sb)
+        widen(4, PLANES[1:2], VECTOR)
+        quant_freq(4, 2)
+        quant_basis(3, GP_FROM, CH)
         widen(4, (2,), VECTOR)
-        quant_freq(6)
-        quant_freq(7)
+        quant_freq(6, 2)
+        quant_basis(3, 0, GP_FROM)
         widen(4, (3,), VECTOR)
-        quant_basis(3)
+        quant_basis(2)
 
         sines(1, PLANES)
         interleave_tensor(4)
@@ -410,8 +473,7 @@ def tile_additive_sine_synthesis_s7_kernel(
         widen(6, (3,), SCALAR)
         window_with_basis(1)
         widen(6, (0, 1, 2), VECTOR)
-        quant_mix(0)
-        quant_mix(1)
+        quant_mix(0, 2)
         quant_basis(5, 0, GP_FROM)
         quant_basis(5, GP_FROM, CH)
         quant_wave(1, 0, CH)
@@ -428,16 +490,16 @@ def tile_additive_sine_synthesis_s7_kernel(
         sines(4, (2, 3))
         window_with_basis(2)
         widen(7, (0, 1, 2), VECTOR)
-        quant_mix(2)
-        quant_mix(3)
+        quant_mix(2, 2)
         quant_basis(6, 0, GP_FROM)
         quant_basis(6, GP_FROM, CH)
         quant_wave(2, 0, CH)
 
         store(0, (0,), 0, CH, SCALAR)
         store(0, (1,), 0, CH, SCALAR)
-        sines(5, (0, 1))
+        sines(5, (0,))
         interleave_tensor(7)
+        sines(5, (1,))
         mix_and_store(0, (2,), 0, CH)
         sines(5, (2, 3))
         mix_and_store(0, (3,), 0, CH)
@@ -454,16 +516,15 @@ def tile_additive_sine_synthesis_s7_kernel(
         sines(6, PLANES)
         window_with_share(4)
         store(1, (1,), 0, CH, VECTOR)
+        sines(7, (0,))
         mix_close(1, (2,), 0, CH)
+        sines(7, (1, 2, 3))
         mix_close(1, (3,), 0, CH)
-        store(1, (3,), 0, CH, SCALAR)
-        sines(7, PLANES)
         quant_shared(4)
         window_with_share(5)
         store(1, (2,), 0, CH, VECTOR)
-
+        store(1, (3,), 0, CH, SCALAR)
         quant_shared(5)
-
         for m in range(MIX_TILES):
             mix_and_store(2, (m,), 0, CH)
         amplify_gpsimd(6, MAIN)

@@ -30,6 +30,7 @@ TURNED_BUFS = 3
 GP_AMP_FROM = {4: 336, 5: 336, 6: 288}
 LAST = 384
 MAIN = 256
+SHIFT = 16
 VECTOR, SCALAR = "vector", "scalar"
 
 
@@ -51,12 +52,17 @@ def tile_additive_sine_synthesis_s7_kernel(
         amp_sb = keep.tile([PART, 2, 4], BF16, name="amp_sb")
         freq_rows = [keep.tile([PART, K], BF16, name="freq_rows%d" % i, align_bytes=64) for i in range(FREQ_TILES)]
         mix_rows = [keep.tile([PART, P], BF16, name="mix_rows%d" % m, align_bytes=64) for m in range(MIX_TILES)]
-        freq_codes = keep.tile([PART, FREQ_TILES, 2 * PART], U32, name="freq_codes", align_bytes=64)
-        freq_scales = keep.tile([PART, FREQ_TILES, 2 * PART], U8, name="freq_scales", align_bytes=64)
-        mix_codes = keep.tile([PART, MIX_TILES, 2 * PART], U32, name="mix_codes", align_bytes=64)
-        mix_scales = keep.tile([PART, MIX_TILES, 2 * PART], U8, name="mix_scales", align_bytes=64)
-        basis_codes = keep.tile([PART, HALVES, CH], U32, name="basis_codes", align_bytes=64)
-        basis_scales = keep.tile([PART, HALVES, CH], U8, name="basis_scales", align_bytes=64)
+
+        def stationary_codes(name, tiles):
+            flat = keep.tile([PART, SHIFT + tiles * 2 * PART], U32, name=name, align_bytes=256)
+            return flat[:, SHIFT:].rearrange("p (i r) -> p i r", i=tiles)
+
+        freq_codes = stationary_codes("freq_codes", FREQ_TILES)
+        freq_scales = keep.tile([PART, FREQ_TILES, 2 * PART], U8, name="freq_scales", align_bytes=256)
+        mix_codes = stationary_codes("mix_codes", MIX_TILES)
+        mix_scales = keep.tile([PART, MIX_TILES, 2 * PART], U8, name="mix_scales", align_bytes=256)
+        basis_codes = keep.tile([PART, HALVES, CH], U32, name="basis_codes", align_bytes=256)
+        basis_scales = keep.tile([PART, HALVES, CH], U8, name="basis_scales", align_bytes=256)
 
         basis_v = basis_bytes.rearrange("(g p t) n -> g p t n", p=PART, t=4)
         freq_v = freq.rearrange("(g m t) k -> g t m k", m=PART, t=4)
@@ -318,9 +324,9 @@ def tile_additive_sine_synthesis_s7_kernel(
 
         def quant_wave(h, n0, n1):
             if h not in wave_codes:
-                wave_codes[h] = work.tile([PART, CH], U32, name="wave_codes", tag="wave_codes", align_bytes=64, bufs=4)
+                wave_codes[h] = work.tile([PART, CH], U32, name="wave_codes", tag="wave_codes", align_bytes=256, bufs=4)
                 wave_scales[h] = work.tile(
-                    [PART, CH], U8, name="wave_scales", tag="wave_scales", align_bytes=64, bufs=4
+                    [PART, CH], U8, name="wave_scales", tag="wave_scales", align_bytes=256, bufs=4
                 )
             nc.vector.quantize_mx(
                 out=wave_codes[h][:, n0:n1].bitcast(FP8X4),

@@ -29,6 +29,7 @@ GP_FROM = 128
 TURNED_BUFS = 3
 GP_AMP_FROM = {4: 336, 5: 336, 6: 288}
 LAST = 384
+LAST_SHARE = 448
 MAIN = 256
 SHIFT = 16
 VECTOR, SCALAR = "vector", "scalar"
@@ -79,6 +80,11 @@ def tile_additive_sine_synthesis_s7_kernel(
         turned = {}
         sine = {}
         wave_in = {}
+        relay = keep.tile([PART, CH + sum(GP_AMP_FROM.values()), 4], BF16, name="relay", align_bytes=64)
+        for h in range(min(GP_AMP_FROM) - 1, max(GP_AMP_FROM) + 1):
+            first = sum(share for later, share in GP_AMP_FROM.items() if later > h)
+            wave_in[h] = relay[:, first : first + CH, :]
+        last = keep.tile([PART, LAST_SHARE - LAST + MAIN, 4], BF16, name="last", align_bytes=64)
         wave_codes = {}
         wave_scales = {}
         sums = {}
@@ -183,35 +189,14 @@ def tile_additive_sine_synthesis_s7_kernel(
             )
             give_bank(("basis", b))
 
-        def interleave_rest(b):
-            basis_in[b, 0] = work.tile([PART, GP_FROM, 4], BF16, name="basis_pe", tag="basis_pe", align_bytes=64)
-            nc.vector.tensor_copy(
-                out=by_four(basis_in[b, 0][:].rearrange("p n t -> p t n")), in_=by_four(wide[b][:, :, :GP_FROM])
-            )
+        def interleave_tensor(b, n0, n1):
+            fill_bank(b, n0, n1)
+            empty_bank(b, n0, n1)
 
-        def interleave_tensor(b):
-            basis_in[b, 0] = work.tile([PART, GP_FROM, 4], BF16, name="basis_pe", tag="basis_pe", align_bytes=64)
-            bank = take_bank(("basis", b), [PART, GP_FROM, 4], BF16)
-            nc.tensor.matmul(
-                bank[:],
-                lhsT=ident_bf[:],
-                rhs=wide[b][:, :, 0:GP_FROM].rearrange("p t n -> p n t"),
-                start=True,
-                stop=True,
-            )
-            nc.scalar.copy(
-                out=basis_in[b, 0][:].rearrange("p n t -> p (n t)").bitcast(F32),
-                in_=bank[:].rearrange("p n t -> p (n t)").bitcast(F32),
-            )
-            give_bank(("basis", b))
-
-        def interleave_gpsimd(b, n0=GP_FROM):
-            basis_in[b, n0] = work.tile(
-                [PART, CH - n0, 4], BF16, name="basis_gp", tag="basis_gp", align_bytes=64, bufs=1
-            )
+        def interleave_gpsimd(b):
             nc.gpsimd.tensor_scalar(
-                out=by_four(basis_in[b, n0][:].rearrange("p n t -> p t n")),
-                in0=by_four(wide[b][:, :, n0:CH]),
+                out=by_four(whole_tile(b)[:, GP_FROM:, :].rearrange("p n t -> p t n")),
+                in0=by_four(wide[b][:, :, GP_FROM:]),
                 scalar1=1.0,
                 scalar2=0.0,
                 op0=MULT,
@@ -293,9 +278,6 @@ def tile_additive_sine_synthesis_s7_kernel(
                 )
                 give_bank(("phase", h, t))
 
-        def relay_tile(h, width):
-            return work.tile([PART, width, 4], BF16, name="relay", tag="relay%d" % h, align_bytes=64, bufs=1)
-
         def product(engine, amp_src, h, dst, n0, n1):
             factor = amp_src[:, h % 2, :].rearrange("p (c t i) -> p c t i", c=1, i=1)
             engine.tensor_tensor(
@@ -305,22 +287,20 @@ def tile_additive_sine_synthesis_s7_kernel(
                 op=MULT,
             )
 
+        def wave_columns(h, n0, n1):
+            if h == HALVES - 1 and n1 <= MAIN:
+                return last[:, LAST_SHARE - LAST + n0 : LAST_SHARE - LAST + n1, :]
+            if h == HALVES - 1 and n0 >= LAST:
+                return last[:, n0 - LAST : n1 - LAST, :]
+            if h not in wave_in:
+                wave_in[h] = work.tile([PART, CH, 4], BF16, name="wave_in", tag="wave_in", align_bytes=64, bufs=2)
+            return wave_in[h][:, n0:n1, :]
+
         def amplify(h, n0, n1):
-            width = n1 - n0
-            if h + 1 in GP_AMP_FROM:
-                wave_in[h, n0] = relay_tile(h + 1, width)
-            else:
-                wave_in[h, n0] = work.tile(
-                    [PART, width, 4], BF16, name="wave_in", tag="wave_in", align_bytes=64, bufs=4
-                )
-            product(nc.vector, factors["amp"], h, wave_in[h, n0][:], n0, n1)
+            product(nc.vector, factors["amp"], h, wave_columns(h, n0, n1), n0, n1)
 
-        def amplify_gpsimd(h, n0, n1=CH):
-            wave_in[h, n0] = relay_tile(h, n1 - n0)
-            product(nc.gpsimd, amp_sb, h, wave_in[h, n0][:, GP_AMP_FROM[h] - n0 :, :], GP_AMP_FROM[h], n1)
-
-        def amplify_rest(h):
-            product(nc.vector, factors["amp"], h, wave_in[h, MAIN][:, : GP_AMP_FROM[h] - MAIN, :], MAIN, GP_AMP_FROM[h])
+        def amplify_gpsimd(h):
+            product(nc.gpsimd, amp_sb, h, wave_in[h][:, GP_AMP_FROM[h] :, :], GP_AMP_FROM[h], CH)
 
         def quant_wave(h, n0, n1):
             if h not in wave_codes:
@@ -331,7 +311,7 @@ def tile_additive_sine_synthesis_s7_kernel(
             nc.vector.quantize_mx(
                 out=wave_codes[h][:, n0:n1].bitcast(FP8X4),
                 scales=wave_scales[h][:, n0:n1],
-                in_=wave_in[h, n0][:].rearrange("p n t -> p (n t)"),
+                in_=wave_columns(h, n0, n1).rearrange("p n t -> p (n t)"),
             )
 
         def mix_pass(dst, m, h, n0, n1, start, stop):
@@ -381,9 +361,8 @@ def tile_additive_sine_synthesis_s7_kernel(
             amplify(h, 0, CH)
 
         def window_with_share(h):
-            amplify_gpsimd(h, MAIN)
-            amplify(h, 0, MAIN)
-            amplify_rest(h)
+            amplify_gpsimd(h)
+            amplify(h, 0, GP_AMP_FROM[h])
 
         def quant_shared(h):
             quant_wave(h, 0, MAIN)
@@ -399,10 +378,14 @@ def tile_additive_sine_synthesis_s7_kernel(
         load_basis(0, slice(1, 4, 2))
         load_basis(1, slice(0, 2))
         load_basis(1, slice(2, 4))
-        load_basis(2)
-        for i in range(4):
-            load_freq(i)
-        load_basis(3)
+        load_basis(2, slice(0, 2))
+        load_basis(2, slice(2, 4))
+        load_freq(0)
+        load_freq(1)
+        load_basis(3, slice(0, 1))
+        load_freq(2)
+        load_freq(3)
+        load_basis(3, slice(1, 4))
         load_by_plane(nc.sync, onset_sb, onset.rearrange("(g p t) -> p g t", p=PART, t=4))
         for i in range(4, FREQ_TILES):
             load_freq(i)
@@ -418,93 +401,90 @@ def tile_additive_sine_synthesis_s7_kernel(
         widen(0, (2, 3), SCALAR)
         widen(1, (0, 1, 2), VECTOR)
         widen(1, (3,), SCALAR)
-        cast(2, 0, 4)
+        cast(2, 0, 2)
+        cast(2, 2, 2)
         warm_tensor(ident, ident[:], ident[:], ident[:])
         factor_to_psum("scale", ident, row_scale)
-        warm_tensor(ident_bf, wide[0][:, 0, :], wide[0][:, 2, :], wide[0][:, 1, :], wide[0][:, 3, :])
-        interleave(0)
-        interleave(1, MAIN)
-        fill_bank(1, MAIN, CH)
-        empty_bank(1, MAIN, CH)
+        warm_tensor(ident_bf, wide[0][:, 0, :], wide[0][:, 2, :])
+        interleave(0, MAIN)
+        interleave(1)
+        interleave_tensor(0, MAIN, CH)
         turn_freq(0)
         turn_freq(1)
+        warm_tensor(ident, ident[:], ident[:])
+        widen(3, PLANES[:1], SCALAR)
         turn_freq(2)
         turn_freq(3)
-        widen(3, (0,), SCALAR)
 
         quant_basis(0)
         quant_basis(1)
         quant_freq(0)
+        widen(3, (1, 2, 3), VECTOR)
         quant_freq(1)
-        widen(3, (1, 2), VECTOR)
-        quant_freq(2)
-        widen(3, (3,), VECTOR)
-        quant_freq(3)
         interleave_gpsimd(3)
         scale_and_interleave(2)
         give_bank("scale")
-        sines(0, (0, 1))
+        sines(0, (0,))
         turn_freq(4)
         turn_freq(5)
-        sines(0, (2,))
+        sines(0, (1,))
         turn_freq(6)
         turn_freq(7)
-        interleave_tensor(3)
+        interleave_tensor(3, 0, GP_FROM)
         widen(4, (0,), SCALAR)
-        sines(0, (3,))
+        quant_freq(2, 2)
+        sines(0, (2, 3))
         factor_to_psum("amp", ident_bf, amp_sb)
         widen(4, PLANES[1:2], VECTOR)
         quant_freq(4, 2)
-        quant_basis(3, GP_FROM, CH)
+        quant_basis(2)
         widen(4, (2,), VECTOR)
         quant_freq(6, 2)
-        quant_basis(3, 0, GP_FROM)
         widen(4, (3,), VECTOR)
-        quant_basis(2)
+        quant_basis(3)
 
         sines(1, PLANES)
-        interleave_tensor(4)
+        interleave_tensor(4, 0, GP_FROM)
         widen(5, (3,), SCALAR)
         window_with_basis(0)
-        widen(5, (0, 1, 2), VECTOR)
-        quant_basis(4, 0, GP_FROM)
-        quant_basis(4, GP_FROM, CH)
+        widen(5, (0, 1), VECTOR)
+        quant_basis(4)
+        widen(5, (2,), VECTOR)
         quant_wave(0, 0, CH)
 
         sines(2, (0, 1))
         turn_mix(0)
         turn_mix(1)
         sines(2, (2, 3))
-        interleave_tensor(5)
-        widen(6, (3,), SCALAR)
+        interleave_tensor(5, 0, GP_FROM)
+        widen(6, (2, 3), SCALAR)
         window_with_basis(1)
-        widen(6, (0, 1, 2), VECTOR)
+        widen(6, (0,), VECTOR)
         quant_mix(0, 2)
-        quant_basis(5, 0, GP_FROM)
-        quant_basis(5, GP_FROM, CH)
+        quant_basis(5)
+        widen(6, (1,), VECTOR)
         quant_wave(1, 0, CH)
 
         sines(3, (0, 1))
         turn_mix(2)
         turn_mix(3)
         sines(3, (2, 3))
-        interleave_tensor(6)
+        interleave_tensor(6, 0, GP_FROM)
         widen(7, (3,), SCALAR)
         sines(4, (0, 1))
         mix_bank(0, (0,), 0, CH)
         mix_bank(0, (1,), 0, CH)
         sines(4, (2, 3))
         window_with_basis(2)
-        widen(7, (0, 1, 2), VECTOR)
+        widen(7, (0, 2), VECTOR)
         quant_mix(2, 2)
-        quant_basis(6, 0, GP_FROM)
-        quant_basis(6, GP_FROM, CH)
+        quant_basis(6)
+        widen(7, (1,), VECTOR)
         quant_wave(2, 0, CH)
 
         store(0, (0,), 0, CH, SCALAR)
         store(0, (1,), 0, CH, SCALAR)
         sines(5, (0,))
-        interleave_tensor(7)
         sines(5, (1,))
         mix_and_store(0, (2,), 0, CH)
         sines(5, (2, 3))
@@ -512,9 +492,9 @@ def tile_additive_sine_synthesis_s7_kernel(
         for m in range(MIX_TILES):
             mix_open(1, (m,), 0, CH)
         window_with_basis(3)
-        quant_basis(7, 0, GP_FROM)
+        interleave(7, GP_FROM)
         quant_wave(3, 0, CH)
-        quant_basis(7, GP_FROM, CH)
+        quant_basis(7)
 
         mix_close(1, (0,), 0, CH)
         store(1, (0,), 0, CH, SCALAR)
@@ -522,9 +502,8 @@ def tile_additive_sine_synthesis_s7_kernel(
         sines(6, PLANES)
         window_with_share(4)
         store(1, (1,), 0, CH, VECTOR)
-        sines(7, (0,))
         mix_close(1, (2,), 0, CH)
-        sines(7, (1, 2, 3))
+        sines(7, PLANES)
         mix_close(1, (3,), 0, CH)
         quant_shared(4)
         window_with_share(5)
@@ -533,19 +512,18 @@ def tile_additive_sine_synthesis_s7_kernel(
         quant_shared(5)
         for m in range(MIX_TILES):
             mix_and_store(2, (m,), 0, CH)
-        amplify_gpsimd(6, MAIN)
-        amplify(6, 0, MAIN)
-        amplify_rest(6)
+        window_with_share(6)
         amplify(7, 0, MAIN)
         quant_wave(6, 0, MAIN)
         quant_wave(7, 0, MAIN)
-        mix_and_store(3, (0, 1), 0, MAIN)
-        mix_and_store(3, (2, 3), 0, MAIN)
+        for m in range(MIX_TILES):
+            mix_and_store(3, (m,), 0, MAIN)
         quant_wave(6, MAIN, CH)
         for m in range(MIX_TILES):
             mix_open(3, (m,), MAIN, CH)
+        product(nc.gpsimd, amp_sb, 7, wave_columns(7, LAST_SHARE, CH), LAST_SHARE, CH)
         amplify(7, MAIN, LAST)
-        amplify(7, LAST, CH)
+        amplify(7, LAST, LAST_SHARE)
         quant_wave(7, MAIN, LAST)
         quant_wave(7, LAST, CH)
         for m in range(MIX_TILES):

@@ -402,13 +402,13 @@ def tile_additive_sine_synthesis_s7_kernel(
         widen(1, (0, 1, 2), VECTOR)
         widen(1, (3,), SCALAR)
         cast(2, 0, 2)
-        cast(2, 2, 2)
         warm_tensor(ident, ident[:], ident[:], ident[:])
         factor_to_psum("scale", ident, row_scale)
         warm_tensor(ident_bf, wide[0][:, 0, :], wide[0][:, 2, :])
         interleave(0, MAIN)
         interleave(1)
         interleave_tensor(0, MAIN, CH)
+        cast(2, 2, 2)
         turn_freq(0)
         turn_freq(1)
         warm_tensor(ident, ident[:], ident[:])

@@ -27,7 +27,7 @@ LEAD = 4
 SINE_BUFS = 4
 GP_FROM = 128
 TURNED_BUFS = 3
-GP_AMP_FROM = {4: 336, 5: 336, 6: 288}
+GP_AMP_FROM = {4: 128, 6: 288}
 LAST = 384
 LAST_SHARE = 448
 MAIN = 256
@@ -81,7 +81,7 @@ def tile_additive_sine_synthesis_s7_kernel(
         sine = {}
         wave_in = {}
         relay = keep.tile([PART, CH + sum(GP_AMP_FROM.values()), 4], BF16, name="relay", align_bytes=64)
-        for h in range(min(GP_AMP_FROM) - 1, max(GP_AMP_FROM) + 1):
+        for h in (3, 4, 6):
             first = sum(share for later, share in GP_AMP_FROM.items() if later > h)
             wave_in[h] = relay[:, first : first + CH, :]
         last = keep.tile([PART, LAST_SHARE - LAST + MAIN, 4], BF16, name="last", align_bytes=64)
@@ -501,15 +501,15 @@ def tile_additive_sine_synthesis_s7_kernel(
         mix_close(1, (1,), 0, CH)
         sines(6, PLANES)
         window_with_share(4)
+        amplify(5, 0, CH)
         store(1, (1,), 0, CH, VECTOR)
         mix_close(1, (2,), 0, CH)
         sines(7, PLANES)
         mix_close(1, (3,), 0, CH)
-        quant_shared(4)
-        window_with_share(5)
         store(1, (2,), 0, CH, VECTOR)
         store(1, (3,), 0, CH, SCALAR)
-        quant_shared(5)
+        quant_wave(4, 0, CH)
+        quant_wave(5, 0, CH)
         for m in range(MIX_TILES):
             mix_and_store(2, (m,), 0, CH)
         window_with_share(6)

from contextlib import ExitStack

import concourse.mybir as mybir
from concourse.masks import make_identity

P, K, T, C = 1024, 1024, 2048, 512
FLOPS = 2 * P * K * T + 2 * C * P * T

F32 = mybir.dt.float32
BF16 = mybir.dt.bfloat16
U32 = mybir.dt.uint32
U8 = mybir.dt.uint8
FP8 = mybir.dt.float8_e4m3fn
FP8X4 = mybir.dt.float8_e4m3fn_x4
MULT = mybir.AluOpType.mult
ADD = mybir.AluOpType.add
ACTF = mybir.ActivationFunctionType

PART = 128
PLANES = range(4)
CH = 512
HALVES = 2 * T // CH
FREQ_TILES = P // PART
MIX_TILES = C // PART
RING_BANKS = 8
LEAD = 4
SINE_BUFS = 4
GP_FROM = 128
TURNED_BUFS = 3
GP_AMP_FROM = {4: 128, 6: 288}
LAST = 384
LAST_SHARE = 448
MAIN = 256
SHIFT = 16
VECTOR, SCALAR = "vector", "scalar"


def tile_additive_sine_synthesis_s7_kernel(
    tc, freq, basis_bytes, basis_scale, onset, amp, mix, out
):
    nc = tc.nc
    with ExitStack() as ctx:
        keep = ctx.enter_context(tc.tile_pool(name="keep", bufs=1))
        work = ctx.enter_context(tc.tile_pool(name="work", bufs=3))
        psum = ctx.enter_context(tc.psum_pool(name="psum", bufs=1))
        ctx.enter_context(tc.manual_schedule())

        ident = keep.tile([PART, PART], F32, name="ident")
        ident_bf = keep.tile([PART, PART], BF16, name="ident_bf")
        table_warm = keep.tile([PART, 1], F32, name="table_warm")
        row_scale = keep.tile([PART, 2, 4], F32, name="row_scale")
        onset_sb = keep.tile([PART, 2, 4], BF16, name="onset_sb")
        amp_sb = keep.tile([PART, 2, 4], BF16, name="amp_sb")
        freq_rows = [keep.tile([PART, K], BF16, name="freq_rows%d" % i, align_bytes=64) for i in range(FREQ_TILES)]
        mix_rows = [keep.tile([PART, P], BF16, name="mix_rows%d" % m, align_bytes=64) for m in range(MIX_TILES)]

        def stationary_codes(name, tiles):
            flat = keep.tile([PART, SHIFT + tiles * 2 * PART], U32, name=name, align_bytes=256)
            return flat[:, SHIFT:].rearrange("p (i r) -> p i r", i=tiles)

        freq_codes = stationary_codes("freq_codes", FREQ_TILES)
        freq_scales = keep.tile([PART, FREQ_TILES, 2 * PART], U8, name="freq_scales", align_bytes=256)
        mix_codes = stationary_codes("mix_codes", MIX_TILES)
        mix_scales = keep.tile([PART, MIX_TILES, 2 * PART], U8, name="mix_scales", align_bytes=256)
        basis_codes = keep.tile([PART, HALVES, CH], U32, name="basis_codes", align_bytes=256)
        basis_scales = keep.tile([PART, HALVES, CH], U8, name="basis_scales", align_bytes=256)

        basis_v = basis_bytes.rearrange("(g p t) n -> g p t n", p=PART, t=4)
        freq_v = freq.rearrange("(g m t) k -> g t m k", m=PART, t=4)
        mix_v = mix.rearrange("(i m) k -> i m k", m=PART)
        out_v = out.rearrange("(m p) n -> p m n", p=PART)

        factors = {}
        pieces = {}
        raw = {}
        wide = {}
        basis_in = {}
        turn_bank = {}
        basis_bank = {}
        turned = {}
        sine = {}
        wave_in = {}
        relay = keep.tile([PART, CH + sum(GP_AMP_FROM.values()), 4], BF16, name="relay", align_bytes=64)
        for h in (3, 4, 6):
            first = sum(share for later, share in GP_AMP_FROM.items() if later > h)
            wave_in[h] = relay[:, first : first + CH, :]
        last = keep.tile([PART, LAST_SHARE - LAST + MAIN, 4], BF16, name="last", align_bytes=64)
        wave_codes = {}
        wave_scales = {}
        sums = {}

        free_banks = list(range(RING_BANKS))
        bank_of = {}

        def take_bank(key, shape, dtype=F32):
            bank_of[key] = free_banks.pop(0)
            return psum.tile(shape, dtype, name="bank", tag="bank%d" % bank_of[key])

        def give_bank(key):
            free_banks.append(bank_of[key])

        def by_four(ap):
            return ap.rearrange("p t (c i) -> p c t i", i=4)

        def load_basis(b, planes=slice(0, 4)):
            c, g = b // 2, b % 2
            held = PLANES[planes]
            piece = keep.tile([PART, len(held), CH], U8, name="raw%d_%d" % (b, held[0]))
            nc.sync.dma_start(out=piece[:], in_=basis_v[g, :, planes, c * CH : (c + 1) * CH])
            pieces[b, held[0]] = piece
            for j, t in enumerate(held):
                raw[b, t] = piece[:, j, :]

        def load_freq(i):
            nc.sync.dma_start(out=freq_rows[i][:], in_=freq_v[i // 4, i % 4])

        def load_mix(m):
            nc.sync.dma_start(out=mix_rows[m][:], in_=mix_v[m])

        def load_by_plane(queue, dst, src):
            queue.dma_start(out=dst[:], in_=src)

        def widen(b, planes, engine):
            if b not in wide:
                wide[b] = work.tile([PART, 4, CH], BF16, name="wide", tag="wide", align_bytes=64, bufs=4)
            for t in planes:
                src = raw[b, t].bitcast(FP8)
                factor = row_scale[:, b % 2, t : t + 1]
                if engine == VECTOR:
                    nc.vector.tensor_scalar(out=wide[b][:, t, :], in0=src, scalar1=factor, scalar2=None, op0=MULT)
                else:
                    nc.scalar.activation(out=wide[b][:, t, :], in_=src, func=ACTF.Copy, scale=factor)

        def cast(b, first, count):
            if b not in wide:
                wide[b] = work.tile([PART, 4, CH], BF16, name="wide", tag="wide", align_bytes=64, bufs=4)
            nc.scalar.copy(
                out=wide[b][:, first : first + count, :].rearrange("p t n -> p (t n)"),
                in_=pieces[b, first][:].rearrange("p t n -> p (t n)").bitcast(FP8),
            )

        def factor_to_psum(key, identity, src):
            factors[key] = take_bank(key, [PART, 2, 4])
            nc.tensor.matmul(
                factors[key][:].rearrange("p g t -> p (g t)"),
                lhsT=identity[:],
                rhs=src[:].rearrange("p g t -> p (g t)"),
                start=True,
                stop=True,
            )

        def scale_and_interleave(b):
            whole_tile(b)
            factor = factors["scale"][:, b % 2, :].rearrange("p (c t i) -> p c t i", c=1, i=1)
            nc.vector.tensor_tensor(
                out=by_four(basis_in[b, 0][:].rearrange("p n t -> p t n")),
                in0=by_four(wide[b][:]),
                in1=factor.to_broadcast([PART, CH // 4, 4, 4]),
                op=MULT,
            )

        def whole_tile(b):
            if (b, 0) not in basis_in:
                basis_in[b, 0] = work.tile(
                    [PART, CH, 4], BF16, name="basis_in", tag="basis_in", align_bytes=64, bufs=3
                )
            return basis_in[b, 0]

        def interleave(b, n1=CH):
            nc.vector.tensor_copy(
                out=by_four(whole_tile(b)[:, :n1, :].rearrange("p n t -> p t n")), in_=by_four(wide[b][:, :, :n1])
            )

        def fill_bank(b, n0, n1):
            basis_bank[b] = take_bank(("basis", b), [PART, n1 - n0, 4], BF16)
            for n in range(n0, n1, PART):
                nc.tensor.matmul(
                    basis_bank[b][:, n - n0 : n - n0 + PART, :],
                    lhsT=ident_bf[:],
                    rhs=wide[b][:, :, n : n + PART].rearrange("p t n -> p n t"),
                    start=True,
                    stop=True,
                )

        def empty_bank(b, n0, n1):
            nc.scalar.copy(
                out=whole_tile(b)[:, n0:n1, :].rearrange("p n t -> p (n t)").bitcast(F32),
                in_=basis_bank[b][:].rearrange("p n t -> p (n t)").bitcast(F32),
            )
            give_bank(("basis", b))

        def interleave_tensor(b, n0, n1):
            fill_bank(b, n0, n1)
            empty_bank(b, n0, n1)

        def interleave_gpsimd(b):
            nc.gpsimd.tensor_scalar(
                out=by_four(whole_tile(b)[:, GP_FROM:, :].rearrange("p n t -> p t n")),
                in0=by_four(wide[b][:, :, GP_FROM:]),
                scalar1=1.0,
                scalar2=0.0,
                op0=MULT,
                op1=ADD,
            )

        def quant_basis(b, n0=0, n1=CH):
            nc.vector.quantize_mx(
                out=basis_codes[:, b, n0:n1].bitcast(FP8X4),
                scales=basis_scales[:, b, n0:n1],
                in_=basis_in[b, n0][:].rearrange("p n t -> p (n t)"),
            )

        def warm_tensor(identity, *sources):
            bank = take_bank("warm", [PART, CH])
            for src in sources:
                nc.tensor.matmul(bank[:, : src.shape[1]], lhsT=identity[:], rhs=src, start=True, stop=True)
            give_bank("warm")

        def turn(operand, rows, i, engine):
            if i % 2 == 0:
                turned[operand, i // 2] = work.tile(
                    [PART, 2, 2, PART, 4], BF16, name="turned", tag="turned", align_bytes=64, bufs=TURNED_BUFS
                )
            words = rows[i][:].bitcast(F32)
            bank = take_bank((operand, i), [PART, 2, 2, PART])
            for g in range(2):
                for u in range(2):
                    nc.tensor.transpose(bank[:, g, u, :], words[:, 256 * g + u : 256 * (g + 1) : 2], ident[:])
            turn_bank[operand, i] = bank
            if engine is not None:
                empty_turned(operand, i, engine)

        def empty_turned(operand, i, engine):
            bank = turn_bank[operand, i]
            dst = turned[operand, i // 2][:, i % 2].rearrange("p g r t -> p (g r t)").bitcast(F32)
            copy = nc.vector.tensor_copy if engine == VECTOR else nc.scalar.copy
            copy(out=dst.rearrange("p (g r u) -> p g r u", g=2, u=2), in_=bank[:].rearrange("p g u r -> p g r u"))
            give_bank((operand, i))

        def quant_turned(operand, codes, scales, i, count):
            nc.vector.quantize_mx(
                out=codes[:, i : i + count, :].rearrange("p i r -> p (i r)").bitcast(FP8X4),
                scales=scales[:, i : i + count, :].rearrange("p i r -> p (i r)"),
                in_=turned[operand, i // 2][:, i % 2 : i % 2 + count].rearrange("p i g r t -> p (i g r t)"),
            )

        def turn_freq(i, engine=SCALAR):
            turn("freq", freq_rows, i, engine)

        def turn_mix(m, engine=SCALAR):
            turn("mix", mix_rows, m, engine)

        def quant_freq(i, count=1):
            quant_turned("freq", freq_codes, freq_scales, i, count)

        def quant_mix(m, count=1):
            quant_turned("mix", mix_codes, mix_scales, m, count)

        def sines(h, planes, n0=0, n1=CH):
            c, half = h // 2, h % 2
            if h not in sine:
                sine[h] = work.tile([PART, 4, CH], F32, name="sine", tag="sine", bufs=SINE_BUFS)
            for t in planes:
                bank = take_bank(("phase", h, t), [PART, n1 - n0])
                i = 4 * half + t
                for g in range(2):
                    nc.tensor.matmul_mx(
                        out=bank[:],
                        lhsT=freq_codes[:, i, PART * g : PART * (g + 1)].bitcast(FP8X4),
                        lhsT_scale=freq_scales[:, i, PART * g : PART * (g + 1)],
                        rhs=basis_codes[:, 2 * c + g, n0:n1].bitcast(FP8X4),
                        rhs_scale=basis_scales[:, 2 * c + g, n0:n1],
                        start=(g == 0),
                        stop=(g == 1),
                    )
                nc.scalar.activation(
                    out=sine[h][:, t, n0:n1], in_=bank[:], func=ACTF.Sin, bias=onset_sb[:, half, t : t + 1]
                )
                give_bank(("phase", h, t))

        def product(engine, amp_src, h, dst, n0, n1):
            factor = amp_src[:, h % 2, :].rearrange("p (c t i) -> p c t i", c=1, i=1)
            engine.tensor_tensor(
                out=by_four(dst.rearrange("p n t -> p t n")),
                in0=by_four(sine[h][:, :, n0:n1]),
                in1=factor.to_broadcast([PART, (n1 - n0) // 4, 4, 4]),
                op=MULT,
            )

        def wave_columns(h, n0, n1):
            if h == HALVES - 1 and n1 <= MAIN:
                return last[:, LAST_SHARE - LAST + n0 : LAST_SHARE - LAST + n1, :]
            if h == HALVES - 1 and n0 >= LAST:
                return last[:, n0 - LAST : n1 - LAST, :]
            if h not in wave_in:
                wave_in[h] = work.tile([PART, CH, 4], BF16, name="wave_in", tag="wave_in", align_bytes=64, bufs=2)
            return wave_in[h][:, n0:n1, :]

        def amplify(h, n0, n1):
            product(nc.vector, factors["amp"], h, wave_columns(h, n0, n1), n0, n1)

        def amplify_gpsimd(h):
            product(nc.gpsimd, amp_sb, h, wave_in[h][:, GP_AMP_FROM[h] :, :], GP_AMP_FROM[h], CH)

        def quant_wave(h, n0, n1):
            if h not in wave_codes:
                wave_codes[h] = work.tile([PART, CH], U32, name="wave_codes", tag="wave_codes", align_bytes=256, bufs=4)
                wave_scales[h] = work.tile(
                    [PART, CH], U8, name="wave_scales", tag="wave_scales", align_bytes=256, bufs=4
                )
            nc.vector.quantize_mx(
                out=wave_codes[h][:, n0:n1].bitcast(FP8X4),
                scales=wave_scales[h][:, n0:n1],
                in_=wave_columns(h, n0, n1).rearrange("p n t -> p (n t)"),
            )

        def mix_pass(dst, m, h, n0, n1, start, stop):
            g = h % 2
            nc.tensor.matmul_mx(
                out=dst,
                lhsT=mix_codes[:, m, PART * g : PART * (g + 1)].bitcast(FP8X4),
                lhsT_scale=mix_scales[:, m, PART * g : PART * (g + 1)],
                rhs=wave_codes[h][:, n0:n1].bitcast(FP8X4),
                rhs_scale=wave_scales[h][:, n0:n1],
                start=start,
                stop=stop,
            )

        def mix_bank(c, tiles, n0, n1):
            key = (c, tiles, n0)
            sums[key] = take_bank(key, [PART, len(tiles), n1 - n0])
            for j, m in enumerate(tiles):
                mix_pass(sums[key][:, j, :], m, 2 * c, n0, n1, True, False)
                mix_pass(sums[key][:, j, :], m, 2 * c + 1, n0, n1, False, True)

        def mix_open(c, tiles, n0, n1):
            key = (c, tiles, n0)
            sums[key] = take_bank(key, [PART, len(tiles), n1 - n0])
            for j, m in enumerate(tiles):
                mix_pass(sums[key][:, j, :], m, 2 * c, n0, n1, j == 0, False)

        def mix_close(c, tiles, n0, n1):
            for j, m in enumerate(tiles):
                mix_pass(sums[c, tiles, n0][:, j, :], m, 2 * c + 1, n0, n1, False, j == len(tiles) - 1)

        def store(c, tiles, n0, n1, engine):
            res = keep.tile([PART, len(tiles), n1 - n0], F32, name="res%d_%d_%d" % (c, tiles[0], n0))
            if engine == VECTOR:
                nc.vector.tensor_copy(out=res[:], in_=sums[c, tiles, n0][:])
            else:
                nc.scalar.copy(out=res[:], in_=sums[c, tiles, n0][:])
            give_bank((c, tiles, n0))
            nc.sync.dma_start(out=out_v[:, tiles[0] : tiles[-1] + 1, c * CH + n0 : c * CH + n1], in_=res[:])

        def mix_and_store(c, tiles, n0, n1):
            mix_bank(c, tiles, n0, n1)
            store(c, tiles, n0, n1, SCALAR)

        def window_with_basis(h):
            interleave_gpsimd(h + LEAD)
            amplify(h, 0, CH)

        def window_with_share(h):
            amplify_gpsimd(h)
            amplify(h, 0, GP_AMP_FROM[h])

        def quant_shared(h):
            quant_wave(h, 0, MAIN)
            quant_wave(h, MAIN, CH)

        load_by_plane(nc.scalar, row_scale, basis_scale.rearrange("(g p t) o -> p g (t o)", p=PART, t=4))
        nc.gpsimd.memset(table_warm[:], 0.0)
        make_identity(nc, ident[:])
        make_identity(nc, ident_bf[:])
        nc.scalar.activation(out=table_warm[:], in_=table_warm[:], func=ACTF.Sin)
        load_basis(0, slice(0, 1))
        load_basis(0, slice(2, 3))
        load_basis(0, slice(1, 4, 2))
        load_basis(1, slice(0, 2))
        load_basis(1, slice(2, 4))
        load_basis(2, slice(0, 2))
        load_basis(2, slice(2, 4))
        load_freq(0)
        load_freq(1)
        load_basis(3, slice(0, 1))
        load_freq(2)
        load_freq(3)
        load_basis(3, slice(1, 4))
        load_by_plane(nc.sync, onset_sb, onset.rearrange("(g p t) -> p g t", p=PART, t=4))
        for i in range(4, FREQ_TILES):
            load_freq(i)
        load_basis(4)
        load_by_plane(nc.sync, amp_sb, amp.rearrange("(g p t) -> p g t", p=PART, t=4))
        load_basis(5)
        for m in range(MIX_TILES):
            load_mix(m)
        load_basis(6)
        load_basis(7)

        widen(0, (0, 1), VECTOR)
        widen(0, (2, 3), SCALAR)
        widen(1, (0, 1, 2), VECTOR)
        widen(1, (3,), SCALAR)
        cast(2, 0, 2)
        warm_tensor(ident, ident[:], ident[:], ident[:])
        factor_to_psum("scale", ident, row_scale)
        warm_tensor(ident_bf, wide[0][:, 0, :], wide[0][:, 2, :])
        interleave(0, MAIN)
        interleave(1)
        interleave_tensor(0, MAIN, CH)
        cast(2, 2, 2)
        turn_freq(0)
        turn_freq(1)
        warm_tensor(ident, ident[:], ident[:])
        widen(3, PLANES[:1], SCALAR)
        turn_freq(2)
        turn_freq(3)

        quant_basis(0)
        quant_basis(1)
        quant_freq(0)
        widen(3, (1, 2, 3), VECTOR)
        quant_freq(1)
        interleave_gpsimd(3)
        scale_and_interleave(2)
        give_bank("scale")
        sines(0, (0,))
        turn_freq(4)
        turn_freq(5)
        sines(0, (1,))
        turn_freq(6)
        turn_freq(7)
        interleave_tensor(3, 0, GP_FROM)
        widen(4, (0,), SCALAR)
        quant_freq(2, 2)
        sines(0, (2, 3))
        factor_to_psum("amp", ident_bf, amp_sb)
        widen(4, PLANES[1:2], VECTOR)
        quant_freq(4, 2)
        quant_basis(2)
        widen(4, (2,), VECTOR)
        quant_freq(6, 2)
        widen(4, (3,), VECTOR)
        quant_basis(3)

        sines(1, PLANES)
        interleave_tensor(4, 0, GP_FROM)
        widen(5, (3,), SCALAR)
        window_with_basis(0)
        widen(5, (0, 1), VECTOR)
        quant_basis(4)
        widen(5, (2,), VECTOR)
        quant_wave(0, 0, CH)

        sines(2, (0, 1))
        turn_mix(0)
        turn_mix(1)
        sines(2, (2, 3))
        interleave_tensor(5, 0, GP_FROM)
        widen(6, (2, 3), SCALAR)
        window_with_basis(1)
        widen(6, (0,), VECTOR)
        quant_mix(0, 2)
        quant_basis(5)
        widen(6, (1,), VECTOR)
        quant_wave(1, 0, CH)

        sines(3, (0, 1))
        turn_mix(2)
        turn_mix(3)
        sines(3, (2, 3))
        interleave_tensor(6, 0, GP_FROM)
        widen(7, (3,), SCALAR)
        sines(4, (0, 1))
        mix_bank(0, (0,), 0, CH)
        mix_bank(0, (1,), 0, CH)
        sines(4, (2, 3))
        window_with_basis(2)
        widen(7, (0, 2), VECTOR)
        quant_mix(2, 2)
        quant_basis(6)
        widen(7, (1,), VECTOR)
        quant_wave(2, 0, CH)

        store(0, (0,), 0, CH, SCALAR)
        store(0, (1,), 0, CH, SCALAR)
        sines(5, (0,))
        sines(5, (1,))
        mix_and_store(0, (2,), 0, CH)
        sines(5, (2, 3))
        mix_and_store(0, (3,), 0, CH)
        for m in range(MIX_TILES):
            mix_open(1, (m,), 0, CH)
        window_with_basis(3)
        interleave(7, GP_FROM)
        quant_wave(3, 0, CH)
        quant_basis(7)

        mix_close(1, (0,), 0, CH)
        store(1, (0,), 0, CH, SCALAR)
        mix_close(1, (1,), 0, CH)
        sines(6, PLANES)
        window_with_share(4)
        amplify(5, 0, CH)
        store(1, (1,), 0, CH, VECTOR)
        mix_close(1, (2,), 0, CH)
        sines(7, PLANES)
        mix_close(1, (3,), 0, CH)
        store(1, (2,), 0, CH, VECTOR)
        store(1, (3,), 0, CH, SCALAR)
        quant_wave(4, 0, CH)
        quant_wave(5, 0, CH)
        for m in range(MIX_TILES):
            mix_and_store(2, (m,), 0, CH)
        window_with_share(6)
        amplify(7, 0, MAIN)
        quant_wave(6, 0, MAIN)
        quant_wave(7, 0, MAIN)
        for m in range(MIX_TILES):
            mix_and_store(3, (m,), 0, MAIN)
        quant_wave(6, MAIN, CH)
        for m in range(MIX_TILES):
            mix_open(3, (m,), MAIN, CH)
        product(nc.gpsimd, amp_sb, 7, wave_columns(7, LAST_SHARE, CH), LAST_SHARE, CH)
        amplify(7, MAIN, LAST)
        amplify(7, LAST, LAST_SHARE)
        quant_wave(7, MAIN, LAST)
        quant_wave(7, LAST, CH)
        for m in range(MIX_TILES):
            mix_close(3, (m,), MAIN, CH)
            store(3, (m,), MAIN, CH, VECTOR if m % 2 == 0 else SCALAR)
